import numpy as np
import ml_dtypes


def mxq(x, axis, fmt="e4m3"):
    dtype, down = {"e4m3": (ml_dtypes.float8_e4m3fn, 7), "e5m2": (ml_dtypes.float8_e5m2, 14)}[fmt]
    v = np.moveaxis(np.asarray(x, np.float32).astype(ml_dtypes.bfloat16).astype(np.float64), axis, -1)
    blocks = v.reshape(v.shape[:-1] + (-1, 32))
    amax = np.abs(blocks).max(-1, keepdims=True)
    byte = np.maximum(np.where(amax > 0, np.frexp(amax)[1] - 1 + 127, 0) - down, 1)
    scale = np.exp2(byte - 127.0)
    codes = (blocks / scale).astype(np.float32).astype(dtype).astype(np.float64)
    return np.moveaxis((codes * scale).reshape(v.shape), -1, axis)


WIDE = False


def mx_kscale(k):
    if not WIDE:
        return np.ones(k)
    levels = np.array([24, -24, 12, -12, 0])
    if k % 512:
        return np.exp2(np.random.permutation(np.resize(levels, k // 32))).repeat(32)
    a = np.empty((k // 512, 16))
    for p in range(k // 512):
        a[p, :8] = np.random.permutation(np.resize(levels, 8))
        for g in range(8):
            far = levels[np.abs(levels - a[p, g]) >= 10]
            a[p, g + 8] = far[np.random.randint(len(far))]
    return np.exp2(a.ravel()).repeat(32)


def f64(x):
    return np.asarray(x).astype(np.float64)


def striped(idx):
    return np.tile(idx.reshape(-1, 16).T, (8, 1)).astype(np.uint16)


def unstriped(offs):
    return offs[:16].T.reshape(-1).astype(np.int64)


E2M1 = np.array([0.0, 0.5, 1.0, 1.5, 2.0, 3.0, 4.0, 6.0, -0.0, -0.5, -1.0, -1.5, -2.0, -3.0, -4.0, -6.0])


def pack_weight(w, fmt):
    k, n = w.shape
    w = f64(np.asarray(w, np.float32).astype(ml_dtypes.bfloat16)).reshape(k // 32, 32, n)
    amax = np.abs(w).max(1)
    if fmt == "e4m3":
        byte = np.frexp(amax)[1] - 1 + 127 - 7
    else:
        mant, ex = np.frexp(amax / 6.0)
        byte = np.where(mant > 0.5, ex, ex - 1) + 127
    byte = np.clip(np.where(amax > 0, byte, 1), 1, 254)
    scaled = (w * np.exp2(127.0 - byte)[:, None, :]).reshape(k, n).astype(np.float32)
    by_word = np.ascontiguousarray(scaled.reshape(k // 512, 128, 4, n).transpose(0, 1, 3, 2))
    if fmt == "e4m3":
        words = by_word.astype(ml_dtypes.float8_e4m3fn).view(np.uint8)
    else:
        c = by_word.astype(ml_dtypes.float4_e2m1fn).view(np.uint8) & 0xF
        words = (c[..., 0::2] | (c[..., 1::2] << 4)).reshape(k // 512, 128, 2 * n)
    return np.ascontiguousarray(words), np.ascontiguousarray(byte.astype(np.uint8).reshape(k // 512, 16, n))


def unpack_weight(words, scales, fmt):
    g, _, n = scales.shape
    words = np.ascontiguousarray(words).reshape(g, 128, n, -1)
    if fmt == "e4m3":
        vals = words.view(ml_dtypes.float8_e4m3fn).astype(np.float64)
    else:
        nib = np.empty((g, 128, n, 4), np.uint8)
        nib[..., 0::2] = words & 0xF
        nib[..., 1::2] = words >> 4
        vals = E2M1[nib]
    vals = vals * np.repeat(np.exp2(scales.astype(np.float64) - 127.0), 8, axis=1)[..., None]
    return vals.transpose(0, 1, 3, 2).reshape(g * 512, n)


def sigm(f):
    return 1.0 / (1.0 + np.exp(-np.maximum(f, -700.0)))


K, N, T, J = 1024, 256, 1024, 512


def setup_inputs():
    n = np.random.standard_normal
    s = mx_kscale(K)[:, None]
    p_tab = pack_weight(n((K, T)) * s, "e4m3")
    p_wk = pack_weight(n((K, N)) / np.sqrt(K) / s, "e2m1")
    p_wv4 = pack_weight(n((K, N)) / np.sqrt(K) / s, "e2m1")
    return {
        "tab_words": p_tab[0],
        "tab_scales": p_tab[1],
        "wk_words": p_wk[0],
        "wk_scales": p_wk[1],
        "wv4_words": p_wv4[0],
        "wv4_scales": p_wv4[1],
        "wvd": (0.4 * (n((K, N)) / np.sqrt(K) / s)).astype(np.float32),
        "st": (n((N, J))).astype(np.float32),
        "rT": (n((N, T))).astype(np.float32),
        "offs": striped(np.random.permutation(T)[:J]),
    }


def reference(tab_words, tab_scales, wk_words, wk_scales, wv4_words, wv4_scales, wvd, st, rT, offs):
    idx = unstriped(offs)
    tab_ = unpack_weight(tab_words, tab_scales, "e4m3")[:, idx]
    wk_ = unpack_weight(wk_words, wk_scales, "e2m1")
    wv4_ = unpack_weight(wv4_words, wv4_scales, "e2m1")
    wvd_ = mxq(f64(wvd), 0, "e4m3")
    ke = wk_.T @ tab_
    ve = wv4_.T @ tab_ + wvd_.T @ tab_
    gate = sigm(ke * f64(st))
    return f64(rT)[:, idx] + gate * ve

@@ -1,0 +1,176 @@
+from contextlib import ExitStack
+
+import concourse.mybir as mybir
+
+K, N, T, J = 1024, 256, 1024, 512
+FLOPS = 3 * 2 * K * N * J
+
+F32 = mybir.dt.float32
+BF16 = mybir.dt.bfloat16
+I32 = mybir.dt.int32
+U32 = mybir.dt.uint32
+U16 = mybir.dt.uint16
+U8 = mybir.dt.uint8
+FP8X4 = mybir.dt.float8_e4m3fn_x4
+FP4X4 = mybir.dt.float4_e2m1fn_x4
+MULT = mybir.AluOpType.mult
+ADD = mybir.AluOpType.add
+SIGMOID = mybir.ActivationFunctionType.Sigmoid
+
+P = 128
+PACK = 4
+K_PASS = P * PACK
+PASSES = K // K_PASS
+HALVES = N // P
+QUADS = 4
+
+
+def tile_list_engram_dl_sigL_kernel(
+    tc, tab_words, tab_scales, wk_words, wk_scales, wv4_words, wv4_scales, wvd, st, rT, offs, out
+):
+    nc = tc.nc
+    with ExitStack() as ctx:
+        pool = ctx.enter_context(tc.tile_pool(name="pool", bufs=1))
+        psum = ctx.enter_context(tc.psum_pool(name="psum", bufs=1))
+
+        def tile(name, shape, dtype):
+            return pool.tile(shape, dtype, name=name, align_bytes=64)
+
+        def load_scale_rows(engine, plane, scales):
+            for q in range(QUADS):
+                engine.dma_start(
+                    out=plane[32 * q : 32 * q + 4, :, :].bitcast(I32),
+                    in_=scales[:, 4 * q : 4 * q + 4, :].rearrange("a r n -> r a n").bitcast(I32),
+                )
+
+        offsets = pool.tile([P, J // 16], U16, name="offsets")
+        tab_w = [tile(f"tab_w{a}", [P, T], U32) for a in range(PASSES)]
+        tab_s = tile("tab_s", [P, PASSES, T], U8)
+        wk_w = tile("wk_w", [P, PASSES, 2 * N], U8)
+        wk_s = tile("wk_s", [P, PASSES, N], U8)
+        wv4_w = tile("wv4_w", [P, PASSES, 2 * N], U8)
+        wv4_s = tile("wv4_s", [P, PASSES, N], U8)
+        wvd_raw = [tile(f"wvd_raw{a}", [P, PACK, N], F32) for a in range(PASSES)]
+        st_sb = [tile(f"st{h}", [P, J], F32) for h in range(HALVES)]
+        r_sb = [tile(f"r{h}", [P, T], F32) for h in range(HALVES)]
+
+        warm_in = tile("warm_in", [P, 8], F32)
+        warm_out = tile("warm_out", [P, 8], F32)
+        for plane in (tab_s, wk_s, wv4_s):
+            nc.vector.memset(plane[:].rearrange("p a n -> p (a n)").bitcast(I32), 0)
+        nc.gpsimd.memset(warm_in[:], 0.0)
+
+        def load_words(dst, words):
+            nc.sync.dma_start(out=dst[:].bitcast(I32), in_=words.rearrange("a p b -> p a b").bitcast(I32))
+
+        def load_table(a):
+            nc.sync.dma_start(
+                out=tab_w[a][:].bitcast(I32), in_=tab_words[a].rearrange("p t i -> p (t i)").bitcast(I32)
+            )
+
+        def load_wvd(a):
+            rows = wvd[a * K_PASS : (a + 1) * K_PASS, :]
+            nc.sync.dma_start(out=wvd_raw[a][:], in_=rows.rearrange("(p t) n -> p t n", t=PACK))
+
+        nc.sync.dma_start(offsets[:], offs)
+        load_scale_rows(nc.scalar, tab_s, tab_scales)
+        load_table(0)
+        load_table(1)
+        load_wvd(0)
+        nc.scalar.activation(warm_out[:], warm_in[:], SIGMOID)
+        load_scale_rows(nc.scalar, wk_s, wk_scales)
+        load_words(wk_w, wk_words)
+        nc.sync.dma_start(out=r_sb[0][:], in_=rT[0:P, :])
+        load_wvd(1)
+        load_scale_rows(nc.scalar, wv4_s, wv4_scales)
+        nc.sync.dma_start(out=st_sb[0][:], in_=st[0:P, :])
+        load_words(wv4_w, wv4_words)
+        nc.sync.dma_start(out=st_sb[1][:], in_=st[P : 2 * P, :])
+        nc.sync.dma_start(out=r_sb[1][:], in_=rT[P : 2 * P, :])
+
+        got_w = [tile(f"got_w{a}", [P, J], U32) for a in range(PASSES)]
+        got_s = [tile(f"got_s{a}", [P, J], U8) for a in range(PASSES)]
+        nc.vector.tensor_copy(got_s[0][:], tab_s[:, 0, :].indirect(offsets[:]))
+        nc.vector.tensor_copy(got_w[0][:], tab_w[0][:].indirect(offsets[:]))
+        nc.vector.tensor_copy(got_s[1][:], tab_s[:, 1, :].indirect(offsets[:]))
+        nc.vector.tensor_copy(got_w[1][:], tab_w[1][:].indirect(offsets[:]))
+
+        wvd_w = [[tile(f"wvd_w{a}{h}", [P, P], U32) for h in range(HALVES)] for a in range(PASSES)]
+        wvd_s = [[tile(f"wvd_s{a}{h}", [P, P], U8) for h in range(HALVES)] for a in range(PASSES)]
+
+        def quantize(a, h):
+            grouped = tile(f"grouped{a}{h}", [P, P, PACK], BF16)
+            nc.scalar.copy(
+                out=grouped[:].rearrange("p (c i) t -> p c t i", i=4),
+                in_=wvd_raw[a][:, :, h * P : (h + 1) * P].rearrange("p t (c i) -> p c t i", i=4),
+            )
+            nc.vector.quantize_mx(
+                out=wvd_w[a][h][:].bitcast(FP8X4),
+                scales=wvd_s[a][h][:],
+                in_=grouped[:].rearrange("p n t -> p (n t)"),
+            )
+
+        ke = [psum.tile([P, J], F32, name=f"ke{h}") for h in range(HALVES)]
+        ve = [psum.tile([P, J], F32, name=f"ve{h}") for h in range(HALVES)]
+
+        def fp4_pass(acc, words, scales, a, h, start, stop):
+            nc.tensor.matmul_mx(
+                out=acc[:],
+                lhsT=words[:, a, 2 * h * P : 2 * (h + 1) * P].bitcast(FP4X4),
+                lhsT_scale=scales[:, a, h * P : (h + 1) * P],
+                rhs=got_w[a][:].bitcast(FP8X4),
+                rhs_scale=got_s[a][:],
+                start=start,
+                stop=stop,
+            )
+
+        def fp8_pass(a, h, start, stop):
+            nc.tensor.matmul_mx(
+                out=ve[h][:],
+                lhsT=wvd_w[a][h][:].bitcast(FP8X4),
+                lhsT_scale=wvd_s[a][h][:],
+                rhs=got_w[a][:].bitcast(FP8X4),
+                rhs_scale=got_s[a][:],
+                start=start,
+                stop=stop,
+            )
+
+        for h in range(HALVES):
+            for a in range(PASSES):
+                fp4_pass(ke[h], wk_w, wk_s, a, h, a == 0, a == PASSES - 1)
+
+        r_got0 = tile("r_got0", [P, J], F32)
+        nc.vector.tensor_copy(r_got0[:], r_sb[0][:].indirect(offsets[:]))
+        for h in range(HALVES):
+            quantize(0, h)
+            fp8_pass(0, h, True, False)
+
+        gate = [tile(f"gate{h}", [P, J], F32) for h in range(HALVES)]
+
+        def make_gate(h):
+            logit = tile(f"logit{h}", [P, J], F32)
+            nc.vector.tensor_tensor(logit[:], ke[h][:], st_sb[h][:], MULT)
+            nc.scalar.activation(gate[h][:], logit[:], SIGMOID)
+
+        make_gate(0)
+        for h in range(HALVES):
+            quantize(1, h)
+        make_gate(1)
+        for h in range(HALVES):
+            for a in range(PASSES):
+                fp4_pass(ve[h], wv4_w, wv4_s, a, h, False, False)
+            fp8_pass(1, h, False, True)
+
+        gated = [tile(f"gated{h}", [P, J], F32) for h in range(HALVES)]
+        for h in range(HALVES):
+            nc.vector.tensor_tensor(gated[h][:], ve[h][:], gate[h][:], MULT)
+        res0 = tile("res0", [P, J], F32)
+        nc.vector.tensor_tensor(res0[:], r_got0[:], gated[0][:], ADD)
+        nc.sync.dma_start(out=out[0:P, :], in_=res0[:])
+        for c in range(2):
+            cols = slice(c * J // 2, (c + 1) * J // 2)
+            res1 = tile(f"res1{c}", [P, J // 2], F32)
+            nc.vector.tensor_tensor(
+                res1[:], r_sb[1][:].indirect(offsets[:, c * 16 : (c + 1) * 16]), gated[1][:, cols], ADD
+            )
+            nc.sync.dma_start(out=out[P : 2 * P, cols], in_=res1[:])

@@ -51,14 +51,14 @@ def tile_list_engram_dl_sigL_kernel(
         wv4_w = tile("wv4_w", [P, PASSES, 2 * N], U8)
         wv4_s = tile("wv4_s", [P, PASSES, N], U8)
         wvd_raw = [tile(f"wvd_raw{a}", [P, PACK, N], F32) for a in range(PASSES)]
-        st_sb = [tile(f"st{h}", [P, J], F32) for h in range(HALVES)]
+        st_sb = tile("st", [P, HALVES, J], F32)
         r_sb = [tile(f"r{h}", [P, T], F32) for h in range(HALVES)]
 
         warm_in = tile("warm_in", [P, 8], F32)
         warm_out = tile("warm_out", [P, 8], F32)
-        for plane in (tab_s, wk_s, wv4_s):
-            nc.vector.memset(plane[:].rearrange("p a n -> p (a n)").bitcast(I32), 0)
-        nc.gpsimd.memset(warm_in[:], 0.0)
+        for engine, plane in ((nc.vector, tab_s), (nc.gpsimd, wk_s), (nc.gpsimd, wv4_s)):
+            engine.memset(plane[:].rearrange("p a n -> p (a n)").bitcast(I32), 0)
+        nc.vector.memset(warm_in[:], 0.0)
 
         def load_words(dst, words):
             nc.sync.dma_start(out=dst[:].bitcast(I32), in_=words.rearrange("a p b -> p a b").bitcast(I32))
@@ -72,41 +72,40 @@ def tile_list_engram_dl_sigL_kernel(
             rows = wvd[a * K_PASS : (a + 1) * K_PASS, :]
             nc.sync.dma_start(out=wvd_raw[a][:], in_=rows.rearrange("(p t) n -> p t n", t=PACK))
 
-        nc.sync.dma_start(offsets[:], offs)
-        load_scale_rows(nc.scalar, tab_s, tab_scales)
         load_table(0)
+        nc.sync.dma_start(offsets[:], offs)
+        load_scale_rows(nc.sync, tab_s, tab_scales)
         load_table(1)
         load_wvd(0)
         nc.scalar.activation(warm_out[:], warm_in[:], SIGMOID)
-        load_scale_rows(nc.scalar, wk_s, wk_scales)
         load_words(wk_w, wk_words)
-        nc.sync.dma_start(out=r_sb[0][:], in_=rT[0:P, :])
-        load_wvd(1)
-        load_scale_rows(nc.scalar, wv4_s, wv4_scales)
-        nc.sync.dma_start(out=st_sb[0][:], in_=st[0:P, :])
         load_words(wv4_w, wv4_words)
-        nc.sync.dma_start(out=st_sb[1][:], in_=st[P : 2 * P, :])
-        nc.sync.dma_start(out=r_sb[1][:], in_=rT[P : 2 * P, :])
+        load_scale_rows(nc.sync, wk_s, wk_scales)
+        load_wvd(1)
+        nc.sync.dma_start(out=st_sb[:], in_=st.rearrange("(h p) j -> p h j", p=P))
+        load_scale_rows(nc.sync, wv4_s, wv4_scales)
+        for h in range(HALVES):
+            nc.sync.dma_start(out=r_sb[h][:], in_=rT[h * P : (h + 1) * P, :])
 
         got_w = [tile(f"got_w{a}", [P, J], U32) for a in range(PASSES)]
         got_s = [tile(f"got_s{a}", [P, J], U8) for a in range(PASSES)]
-        nc.vector.tensor_copy(got_s[0][:], tab_s[:, 0, :].indirect(offsets[:]))
         nc.vector.tensor_copy(got_w[0][:], tab_w[0][:].indirect(offsets[:]))
-        nc.vector.tensor_copy(got_s[1][:], tab_s[:, 1, :].indirect(offsets[:]))
+        nc.vector.tensor_copy(got_s[0][:], tab_s[:, 0, :].indirect(offsets[:]))
         nc.vector.tensor_copy(got_w[1][:], tab_w[1][:].indirect(offsets[:]))
+        nc.vector.tensor_copy(got_s[1][:], tab_s[:, 1, :].indirect(offsets[:]))
 
-        wvd_w = [[tile(f"wvd_w{a}{h}", [P, P], U32) for h in range(HALVES)] for a in range(PASSES)]
-        wvd_s = [[tile(f"wvd_s{a}{h}", [P, P], U8) for h in range(HALVES)] for a in range(PASSES)]
+        wvd_w = [tile(f"wvd_w{a}", [P, N], U32) for a in range(PASSES)]
+        wvd_s = [tile(f"wvd_s{a}", [P, N], U8) for a in range(PASSES)]
 
-        def quantize(a, h):
-            grouped = tile(f"grouped{a}{h}", [P, P, PACK], BF16)
+        def quantize(a):
+            grouped = tile(f"grouped{a}", [P, N, PACK], BF16)
             nc.scalar.copy(
                 out=grouped[:].rearrange("p (c i) t -> p c t i", i=4),
-                in_=wvd_raw[a][:, :, h * P : (h + 1) * P].rearrange("p t (c i) -> p c t i", i=4),
+                in_=wvd_raw[a][:].rearrange("p t (c i) -> p c t i", i=4),
             )
             nc.vector.quantize_mx(
-                out=wvd_w[a][h][:].bitcast(FP8X4),
-                scales=wvd_s[a][h][:],
+                out=wvd_w[a][:].bitcast(FP8X4),
+                scales=wvd_s[a][:],
                 in_=grouped[:].rearrange("p n t -> p (n t)"),
             )
 
@@ -127,45 +126,41 @@ def tile_list_engram_dl_sigL_kernel(
         def fp8_pass(a, h, start, stop):
             nc.tensor.matmul_mx(
                 out=ve[h][:],
-                lhsT=wvd_w[a][h][:].bitcast(FP8X4),
-                lhsT_scale=wvd_s[a][h][:],
+                lhsT=wvd_w[a][:, h * P : (h + 1) * P].bitcast(FP8X4),
+                lhsT_scale=wvd_s[a][:, h * P : (h + 1) * P],
                 rhs=got_w[a][:].bitcast(FP8X4),
                 rhs_scale=got_s[a][:],
                 start=start,
                 stop=stop,
             )
 
-        for h in range(HALVES):
-            for a in range(PASSES):
+        for a in range(PASSES):
+            for h in range(HALVES):
                 fp4_pass(ke[h], wk_w, wk_s, a, h, a == 0, a == PASSES - 1)
 
-        r_got0 = tile("r_got0", [P, J], F32)
-        nc.vector.tensor_copy(r_got0[:], r_sb[0][:].indirect(offsets[:]))
-        for h in range(HALVES):
-            quantize(0, h)
-            fp8_pass(0, h, True, False)
+        for a in range(PASSES):
+            quantize(a)
 
         gate = [tile(f"gate{h}", [P, J], F32) for h in range(HALVES)]
 
         def make_gate(h):
             logit = tile(f"logit{h}", [P, J], F32)
-            nc.vector.tensor_tensor(logit[:], ke[h][:], st_sb[h][:], MULT)
+            nc.vector.tensor_tensor(logit[:], ke[h][:], st_sb[:, h, :], MULT)
             nc.scalar.activation(gate[h][:], logit[:], SIGMOID)
 
-        make_gate(0)
         for h in range(HALVES):
-            quantize(1, h)
-        make_gate(1)
+            make_gate(h)
         for h in range(HALVES):
             for a in range(PASSES):
-                fp4_pass(ve[h], wv4_w, wv4_s, a, h, False, False)
-            fp8_pass(1, h, False, True)
+                fp4_pass(ve[h], wv4_w, wv4_s, a, h, a == 0, False)
+            for a in range(PASSES):
+                fp8_pass(a, h, False, a == PASSES - 1)
 
         gated = [tile(f"gated{h}", [P, J], F32) for h in range(HALVES)]
-        for h in range(HALVES):
-            nc.vector.tensor_tensor(gated[h][:], ve[h][:], gate[h][:], MULT)
+        nc.vector.tensor_tensor(gated[0][:], ve[0][:], gate[0][:], MULT)
+        nc.vector.tensor_tensor(gated[1][:], ve[1][:], gate[1][:], MULT)
         res0 = tile("res0", [P, J], F32)
-        nc.vector.tensor_tensor(res0[:], r_got0[:], gated[0][:], ADD)
+        nc.vector.tensor_tensor(res0[:], r_sb[0][:].indirect(offsets[:]), gated[0][:], ADD)
         nc.sync.dma_start(out=out[0:P, :], in_=res0[:])
         for c in range(2):
             cols = slice(c * J // 2, (c + 1) * J // 2)

@@ -37,11 +37,9 @@ def tile_list_engram_dl_sigL_kernel(
             return pool.tile(shape, dtype, name=name, align_bytes=64)
 
         def load_scale_rows(engine, plane, scales):
-            for q in range(QUADS):
-                engine.dma_start(
-                    out=plane[32 * q : 32 * q + 4, :, :].bitcast(I32),
-                    in_=scales[:, 4 * q : 4 * q + 4, :].rearrange("a r n -> r a n").bitcast(I32),
-                )
+            rows = scales.rearrange("a (q r) n -> r q a n", r=4)
+            for r in range(4):
+                engine.dma_start(out=plane[r:P:32, :, :].bitcast(I32), in_=rows[r].bitcast(I32))
 
         offsets = pool.tile([P, J // 16], U16, name="offsets")
         tab_w = [tile(f"tab_w{a}", [P, T], U32) for a in range(PASSES)]
@@ -51,12 +49,14 @@ def tile_list_engram_dl_sigL_kernel(
         wv4_w = tile("wv4_w", [P, PASSES, 2 * N], U8)
         wv4_s = tile("wv4_s", [P, PASSES, N], U8)
         wvd_raw = [tile(f"wvd_raw{a}", [P, PACK, N], F32) for a in range(PASSES)]
-        st_sb = tile("st", [P, HALVES, J], F32)
+        st_sb = [tile(f"st{h}", [P, J], F32) for h in range(HALVES)]
         r_sb = [tile(f"r{h}", [P, T], F32) for h in range(HALVES)]
 
         warm_in = tile("warm_in", [P, 8], F32)
         warm_out = tile("warm_out", [P, 8], F32)
-        for engine, plane in ((nc.vector, tab_s), (nc.gpsimd, wk_s), (nc.gpsimd, wv4_s)):
+        nc.vector.memset(tab_s[:, 0, :].bitcast(I32), 0)
+        nc.gpsimd.memset(tab_s[:, 1, :].bitcast(I32), 0)
+        for engine, plane in ((nc.vector, wk_s), (nc.gpsimd, wv4_s)):
             engine.memset(plane[:].rearrange("p a n -> p (a n)").bitcast(I32), 0)
         nc.vector.memset(warm_in[:], 0.0)
 
@@ -74,16 +74,17 @@ def tile_list_engram_dl_sigL_kernel(
 
         load_table(0)
         nc.sync.dma_start(offsets[:], offs)
+        load_words(wk_w, wk_words)
         load_scale_rows(nc.sync, tab_s, tab_scales)
         load_table(1)
-        load_wvd(0)
         nc.scalar.activation(warm_out[:], warm_in[:], SIGMOID)
-        load_words(wk_w, wk_words)
-        load_words(wv4_w, wv4_words)
+        load_wvd(0)
         load_scale_rows(nc.sync, wk_s, wk_scales)
+        load_words(wv4_w, wv4_words)
         load_wvd(1)
-        nc.sync.dma_start(out=st_sb[:], in_=st.rearrange("(h p) j -> p h j", p=P))
+        nc.sync.dma_start(out=st_sb[0][:], in_=st[0:P, :])
         load_scale_rows(nc.sync, wv4_s, wv4_scales)
+        nc.sync.dma_start(out=st_sb[1][:], in_=st[P : 2 * P, :])
         for h in range(HALVES):
             nc.sync.dma_start(out=r_sb[h][:], in_=rT[h * P : (h + 1) * P, :])
 
@@ -97,15 +98,15 @@ def tile_list_engram_dl_sigL_kernel(
         wvd_w = [tile(f"wvd_w{a}", [P, N], U32) for a in range(PASSES)]
         wvd_s = [tile(f"wvd_s{a}", [P, N], U8) for a in range(PASSES)]
 
-        def quantize(a):
-            grouped = tile(f"grouped{a}", [P, N, PACK], BF16)
+        def quantize(a, n0, n1):
+            grouped = tile(f"grouped{a}_{n0}", [P, n1 - n0, PACK], BF16)
             nc.scalar.copy(
                 out=grouped[:].rearrange("p (c i) t -> p c t i", i=4),
-                in_=wvd_raw[a][:].rearrange("p t (c i) -> p c t i", i=4),
+                in_=wvd_raw[a][:, :, n0:n1].rearrange("p t (c i) -> p c t i", i=4),
             )
             nc.vector.quantize_mx(
-                out=wvd_w[a][:].bitcast(FP8X4),
-                scales=wvd_s[a][:],
+                out=wvd_w[a][:, n0:n1].bitcast(FP8X4),
+                scales=wvd_s[a][:, n0:n1],
                 in_=grouped[:].rearrange("p n t -> p (n t)"),
             )
 
@@ -138,14 +139,15 @@ def tile_list_engram_dl_sigL_kernel(
             for h in range(HALVES):
                 fp4_pass(ke[h], wk_w, wk_s, a, h, a == 0, a == PASSES - 1)
 
-        for a in range(PASSES):
-            quantize(a)
+        quantize(0, 0, N)
+        for h in range(HALVES):
+            quantize(1, h * P, (h + 1) * P)
 
         gate = [tile(f"gate{h}", [P, J], F32) for h in range(HALVES)]
 
         def make_gate(h):
             logit = tile(f"logit{h}", [P, J], F32)
-            nc.vector.tensor_tensor(logit[:], ke[h][:], st_sb[:, h, :], MULT)
+            nc.vector.tensor_tensor(logit[:], ke[h][:], st_sb[h][:], MULT)
             nc.scalar.activation(gate[h][:], logit[:], SIGMOID)
 
         for h in range(HALVES):

@@ -36,14 +36,14 @@ def tile_list_engram_dl_sigL_kernel(
         def tile(name, shape, dtype):
             return pool.tile(shape, dtype, name=name, align_bytes=64)
 
-        def load_scale_rows(engine, plane, scales):
+        def load_scale_rows(plane, scales):
             rows = scales.rearrange("a (q r) n -> r q a n", r=4)
             for r in range(4):
-                engine.dma_start(out=plane[r:P:32, :, :].bitcast(I32), in_=rows[r].bitcast(I32))
+                nc.sync.dma_start(out=plane[r:P:32, :, :].bitcast(I32), in_=rows[r].bitcast(I32))
 
         offsets = pool.tile([P, J // 16], U16, name="offsets")
         tab_w = [tile(f"tab_w{a}", [P, T], U32) for a in range(PASSES)]
-        tab_s = tile("tab_s", [P, PASSES, T], U8)
+        tab_s = tile("tab_s", [P, T], U8)
         wk_w = tile("wk_w", [P, PASSES, 2 * N], U8)
         wk_s = tile("wk_s", [P, PASSES, N], U8)
         wv4_w = tile("wv4_w", [P, PASSES, 2 * N], U8)
@@ -51,14 +51,23 @@ def tile_list_engram_dl_sigL_kernel(
         wvd_raw = [tile(f"wvd_raw{a}", [P, PACK, N], F32) for a in range(PASSES)]
         st_sb = [tile(f"st{h}", [P, J], F32) for h in range(HALVES)]
         r_sb = [tile(f"r{h}", [P, T], F32) for h in range(HALVES)]
+        got_w = [tile(f"got_w{a}", [P, J], U32) for a in range(PASSES)]
+        got_s = [tile(f"got_s{a}", [P, J], U8) for a in range(PASSES)]
 
         warm_in = tile("warm_in", [P, 8], F32)
         warm_out = tile("warm_out", [P, 8], F32)
-        nc.vector.memset(tab_s[:, 0, :].bitcast(I32), 0)
-        nc.gpsimd.memset(tab_s[:, 1, :].bitcast(I32), 0)
-        for engine, plane in ((nc.vector, wk_s), (nc.gpsimd, wv4_s)):
-            engine.memset(plane[:].rearrange("p a n -> p (a n)").bitcast(I32), 0)
+        nc.vector.memset(tab_s[:].bitcast(I32), 0)
+        for plane in (wk_s, wv4_s):
+            nc.vector.memset(plane[:].rearrange("p a n -> p (a n)").bitcast(I32), 0)
+        nc.vector.memset(got_s[1][:].bitcast(I32), 0)
         nc.vector.memset(warm_in[:], 0.0)
+
+        def load_table_scales():
+            for q in range(QUADS):
+                nc.sync.dma_start(
+                    out=tab_s[32 * q : 32 * q + 4 * PASSES, :].bitcast(I32),
+                    in_=tab_scales[:, 4 * q : 4 * q + 4, :].bitcast(I32),
+                )
 
         def load_words(dst, words):
             nc.sync.dma_start(out=dst[:].bitcast(I32), in_=words.rearrange("a p b -> p a b").bitcast(I32))
@@ -72,28 +81,29 @@ def tile_list_engram_dl_sigL_kernel(
             rows = wvd[a * K_PASS : (a + 1) * K_PASS, :]
             nc.sync.dma_start(out=wvd_raw[a][:], in_=rows.rearrange("(p t) n -> p t n", t=PACK))
 
-        load_table(0)
+        def load_rows(tiles, src, h):
+            nc.sync.dma_start(out=tiles[h][:], in_=src[h * P : (h + 1) * P, :])
+
         nc.sync.dma_start(offsets[:], offs)
         load_words(wk_w, wk_words)
-        load_scale_rows(nc.sync, tab_s, tab_scales)
+        load_words(wv4_w, wv4_words)
+        load_table_scales()
+        load_table(0)
         load_table(1)
         nc.scalar.activation(warm_out[:], warm_in[:], SIGMOID)
+        load_scale_rows(wk_s, wk_scales)
         load_wvd(0)
-        load_scale_rows(nc.sync, wk_s, wk_scales)
-        load_words(wv4_w, wv4_words)
         load_wvd(1)
-        nc.sync.dma_start(out=st_sb[0][:], in_=st[0:P, :])
-        load_scale_rows(nc.sync, wv4_s, wv4_scales)
-        nc.sync.dma_start(out=st_sb[1][:], in_=st[P : 2 * P, :])
-        for h in range(HALVES):
-            nc.sync.dma_start(out=r_sb[h][:], in_=rT[h * P : (h + 1) * P, :])
+        load_scale_rows(wv4_s, wv4_scales)
+        load_rows(st_sb, st, 0)
+        load_rows(st_sb, st, 1)
+        load_rows(r_sb, rT, 0)
+        load_rows(r_sb, rT, 1)
 
-        got_w = [tile(f"got_w{a}", [P, J], U32) for a in range(PASSES)]
-        got_s = [tile(f"got_s{a}", [P, J], U8) for a in range(PASSES)]
-        nc.vector.tensor_copy(got_w[0][:], tab_w[0][:].indirect(offsets[:]))
-        nc.vector.tensor_copy(got_s[0][:], tab_s[:, 0, :].indirect(offsets[:]))
-        nc.vector.tensor_copy(got_w[1][:], tab_w[1][:].indirect(offsets[:]))
-        nc.vector.tensor_copy(got_s[1][:], tab_s[:, 1, :].indirect(offsets[:]))
+        nc.vector.tensor_copy(got_s[0][:], tab_s[:].indirect(offsets[:]))
+        nc.scalar.dma_start(out=got_s[1][0:112, :].bitcast(I32), in_=got_s[0][4:116, :].bitcast(I32))
+        for a in range(PASSES):
+            nc.vector.tensor_copy(got_w[a][:], tab_w[a][:].indirect(offsets[:]))
 
         wvd_w = [tile(f"wvd_w{a}", [P, N], U32) for a in range(PASSES)]
         wvd_s = [tile(f"wvd_s{a}", [P, N], U8) for a in range(PASSES)]

@@ -23,6 +23,7 @@ K_PASS = P * PACK
 PASSES = K // K_PASS
 HALVES = N // P
 QUADS = 4
+SPLIT = 128
 
 
 def tile_list_engram_dl_sigL_kernel(
@@ -89,34 +90,33 @@ def tile_list_engram_dl_sigL_kernel(
         load_words(wv4_w, wv4_words)
         load_table_scales()
         load_table(0)
-        load_table(1)
+        load_wvd(0)
         nc.scalar.activation(warm_out[:], warm_in[:], SIGMOID)
         load_scale_rows(wk_s, wk_scales)
-        load_wvd(0)
+        load_table(1)
         load_wvd(1)
+
+        nc.vector.tensor_copy(got_s[0][:], tab_s[:].indirect(offsets[:]))
+        nc.sync.dma_start(out=got_s[1][0:112, :].bitcast(I32), in_=got_s[0][4:116, :].bitcast(I32))
         load_scale_rows(wv4_s, wv4_scales)
         load_rows(st_sb, st, 0)
         load_rows(st_sb, st, 1)
         load_rows(r_sb, rT, 0)
         load_rows(r_sb, rT, 1)
 
-        nc.vector.tensor_copy(got_s[0][:], tab_s[:].indirect(offsets[:]))
-        nc.scalar.dma_start(out=got_s[1][0:112, :].bitcast(I32), in_=got_s[0][4:116, :].bitcast(I32))
-        for a in range(PASSES):
-            nc.vector.tensor_copy(got_w[a][:], tab_w[a][:].indirect(offsets[:]))
-
         wvd_w = [tile(f"wvd_w{a}", [P, N], U32) for a in range(PASSES)]
-        wvd_s = [tile(f"wvd_s{a}", [P, N], U8) for a in range(PASSES)]
+        wvd_s = [wk_s[4:P, 1, :], tile("wvd_s1", [P, N], U8)]
 
-        def quantize(a, n0, n1):
-            grouped = tile(f"grouped{a}_{n0}", [P, n1 - n0, PACK], BF16)
-            nc.scalar.copy(
-                out=grouped[:].rearrange("p (c i) t -> p c t i", i=4),
-                in_=wvd_raw[a][:, :, n0:n1].rearrange("p t (c i) -> p c t i", i=4),
-            )
+        def quantize(a):
+            grouped = tile(f"grouped{a}", [P, N, PACK], BF16)
+            for copy, n0, n1 in ((nc.scalar.copy, 0, SPLIT), (nc.vector.tensor_copy, SPLIT, N)):
+                copy(
+                    out=grouped[:, n0:n1, :].rearrange("p (c i) t -> p c t i", i=4),
+                    in_=wvd_raw[a][:, :, n0:n1].rearrange("p t (c i) -> p c t i", i=4),
+                )
             nc.vector.quantize_mx(
-                out=wvd_w[a][:, n0:n1].bitcast(FP8X4),
-                scales=wvd_s[a][:, n0:n1],
+                out=wvd_w[a][:].bitcast(FP8X4),
+                scales=wvd_s[a][:, :],
                 in_=grouped[:].rearrange("p n t -> p (n t)"),
             )
 
@@ -145,28 +145,32 @@ def tile_list_engram_dl_sigL_kernel(
                 stop=stop,
             )
 
-        for a in range(PASSES):
-            for h in range(HALVES):
-                fp4_pass(ke[h], wk_w, wk_s, a, h, a == 0, a == PASSES - 1)
-
-        quantize(0, 0, N)
+        nc.vector.tensor_copy(got_w[0][:], tab_w[0][:].indirect(offsets[:]))
         for h in range(HALVES):
-            quantize(1, h * P, (h + 1) * P)
+            fp4_pass(ke[h], wk_w, wk_s, 0, h, True, False)
+        quantize(0)
+        for h in range(HALVES):
+            fp8_pass(0, h, True, False)
+        nc.vector.tensor_copy(got_w[1][:], tab_w[1][:].indirect(offsets[:]))
+        for h in range(HALVES):
+            fp4_pass(ke[h], wk_w, wk_s, 1, h, False, True)
+        quantize(1)
 
         gate = [tile(f"gate{h}", [P, J], F32) for h in range(HALVES)]
 
         def make_gate(h):
-            logit = tile(f"logit{h}", [P, J], F32)
-            nc.vector.tensor_tensor(logit[:], ke[h][:], st_sb[h][:], MULT)
-            nc.scalar.activation(gate[h][:], logit[:], SIGMOID)
+            for c in range(2):
+                cols = slice(c * J // 2, (c + 1) * J // 2)
+                logit = tile(f"logit{h}{c}", [P, J // 2], F32)
+                nc.vector.tensor_tensor(logit[:], ke[h][:, cols], st_sb[h][:, cols], MULT)
+                nc.scalar.activation(gate[h][:, cols], logit[:], SIGMOID)
 
         for h in range(HALVES):
             make_gate(h)
         for h in range(HALVES):
             for a in range(PASSES):
-                fp4_pass(ve[h], wv4_w, wv4_s, a, h, a == 0, False)
-            for a in range(PASSES):
-                fp8_pass(a, h, False, a == PASSES - 1)
+                fp4_pass(ve[h], wv4_w, wv4_s, a, h, False, False)
+            fp8_pass(1, h, False, True)
 
         gated = [tile(f"gated{h}", [P, J], F32) for h in range(HALVES)]
         nc.vector.tensor_tensor(gated[0][:], ve[0][:], gate[0][:], MULT)

@@ -23,6 +23,7 @@ K_PASS = P * PACK
 PASSES = K // K_PASS
 HALVES = N // P
 QUADS = 4
+LAST = 128
 SPLIT = 128
 
 
@@ -64,11 +65,9 @@ def tile_list_engram_dl_sigL_kernel(
         nc.vector.memset(warm_in[:], 0.0)
 
         def load_table_scales():
-            for q in range(QUADS):
-                nc.sync.dma_start(
-                    out=tab_s[32 * q : 32 * q + 4 * PASSES, :].bitcast(I32),
-                    in_=tab_scales[:, 4 * q : 4 * q + 4, :].bitcast(I32),
-                )
+            rows = tab_scales.rearrange("a (q r) t -> r q a t", r=4)
+            for r in range(4):
+                nc.sync.dma_start(out=tab_s[r:P:16, :].bitcast(I32), in_=rows[r].bitcast(I32))
 
         def load_words(dst, words):
             nc.sync.dma_start(out=dst[:].bitcast(I32), in_=words.rearrange("a p b -> p a b").bitcast(I32))
@@ -97,7 +96,7 @@ def tile_list_engram_dl_sigL_kernel(
         load_wvd(1)
 
         nc.vector.tensor_copy(got_s[0][:], tab_s[:].indirect(offsets[:]))
-        nc.sync.dma_start(out=got_s[1][0:112, :].bitcast(I32), in_=got_s[0][4:116, :].bitcast(I32))
+        nc.sync.dma_start(out=got_s[1][0:112, :].bitcast(I32), in_=got_s[0][16:P, :].bitcast(I32))
         load_scale_rows(wv4_s, wv4_scales)
         load_rows(st_sb, st, 0)
         load_rows(st_sb, st, 1)
@@ -178,10 +177,10 @@ def tile_list_engram_dl_sigL_kernel(
         res0 = tile("res0", [P, J], F32)
         nc.vector.tensor_tensor(res0[:], r_sb[0][:].indirect(offsets[:]), gated[0][:], ADD)
         nc.sync.dma_start(out=out[0:P, :], in_=res0[:])
-        for c in range(2):
-            cols = slice(c * J // 2, (c + 1) * J // 2)
-            res1 = tile(f"res1{c}", [P, J // 2], F32)
+        for j0, j1 in ((0, J - LAST), (J - LAST, J)):
+            cols = slice(j0, j1)
+            res1 = tile(f"res1_{j0}", [P, j1 - j0], F32)
             nc.vector.tensor_tensor(
-                res1[:], r_sb[1][:].indirect(offsets[:, c * 16 : (c + 1) * 16]), gated[1][:, cols], ADD
+                res1[:], r_sb[1][:].indirect(offsets[:, j0 // 16 : j1 // 16]), gated[1][:, cols], ADD
             )
             nc.sync.dma_start(out=out[P : 2 * P, cols], in_=res1[:])

@@ -158,9 +158,10 @@ def tile_list_engram_dl_sigL_kernel(
         gate = [tile(f"gate{h}", [P, J], F32) for h in range(HALVES)]
 
         def make_gate(h):
-            for c in range(2):
-                cols = slice(c * J // 2, (c + 1) * J // 2)
-                logit = tile(f"logit{h}{c}", [P, J // 2], F32)
+            pieces = 2 - h
+            for c in range(pieces):
+                cols = slice(c * J // pieces, (c + 1) * J // pieces)
+                logit = tile(f"logit{h}{c}", [P, J // pieces], F32)
                 nc.vector.tensor_tensor(logit[:], ke[h][:, cols], st_sb[h][:, cols], MULT)
                 nc.scalar.activation(gate[h][:, cols], logit[:], SIGMOID)
 
@@ -171,16 +172,14 @@ def tile_list_engram_dl_sigL_kernel(
                 fp4_pass(ve[h], wv4_w, wv4_s, a, h, False, False)
             fp8_pass(1, h, False, True)
 
-        gated = [tile(f"gated{h}", [P, J], F32) for h in range(HALVES)]
-        nc.vector.tensor_tensor(gated[0][:], ve[0][:], gate[0][:], MULT)
-        nc.vector.tensor_tensor(gated[1][:], ve[1][:], gate[1][:], MULT)
-        res0 = tile("res0", [P, J], F32)
-        nc.vector.tensor_tensor(res0[:], r_sb[0][:].indirect(offsets[:]), gated[0][:], ADD)
-        nc.sync.dma_start(out=out[0:P, :], in_=res0[:])
-        for j0, j1 in ((0, J - LAST), (J - LAST, J)):
-            cols = slice(j0, j1)
-            res1 = tile(f"res1_{j0}", [P, j1 - j0], F32)
-            nc.vector.tensor_tensor(
-                res1[:], r_sb[1][:].indirect(offsets[:, j0 // 16 : j1 // 16]), gated[1][:, cols], ADD
-            )
-            nc.sync.dma_start(out=out[P : 2 * P, cols], in_=res1[:])
+        gated = tile("gated", [P, J], F32)
+        for h, cuts in enumerate(((0, J // 2, J), (0, J // 2, J - LAST, J))):
+            for c in range(2):
+                cols = slice(c * J // 2, (c + 1) * J // 2)
+                nc.vector.tensor_tensor(gated[:, cols], ve[h][:, cols], gate[h][:, cols], MULT)
+            for j0, j1 in zip(cuts, cuts[1:]):
+                res = tile(f"res{h}_{j0}", [P, j1 - j0], F32)
+                nc.vector.tensor_tensor(
+                    res[:], r_sb[h][:].indirect(offsets[:, j0 // 16 : j1 // 16]), gated[:, j0:j1], ADD
+                )
+                nc.sync.dma_start(out=out[h * P : (h + 1) * P, j0:j1], in_=res[:])

@@ -24,7 +24,6 @@ PASSES = K // K_PASS
 HALVES = N // P
 QUADS = 4
 LAST = 128
-SPLIT = 128
 
 
 def tile_list_engram_dl_sigL_kernel(
@@ -56,13 +55,10 @@ def tile_list_engram_dl_sigL_kernel(
         got_w = [tile(f"got_w{a}", [P, J], U32) for a in range(PASSES)]
         got_s = [tile(f"got_s{a}", [P, J], U8) for a in range(PASSES)]
 
-        warm_in = tile("warm_in", [P, 8], F32)
-        warm_out = tile("warm_out", [P, 8], F32)
         nc.vector.memset(tab_s[:].bitcast(I32), 0)
         for plane in (wk_s, wv4_s):
             nc.vector.memset(plane[:].rearrange("p a n -> p (a n)").bitcast(I32), 0)
         nc.vector.memset(got_s[1][:].bitcast(I32), 0)
-        nc.vector.memset(warm_in[:], 0.0)
 
         def load_table_scales():
             rows = tab_scales.rearrange("a (q r) t -> r q a t", r=4)
@@ -90,7 +86,6 @@ def tile_list_engram_dl_sigL_kernel(
         load_table_scales()
         load_table(0)
         load_wvd(0)
-        nc.scalar.activation(warm_out[:], warm_in[:], SIGMOID)
         load_scale_rows(wk_s, wk_scales)
         load_table(1)
         load_wvd(1)
@@ -107,17 +102,18 @@ def tile_list_engram_dl_sigL_kernel(
         wvd_s = [wk_s[4:P, 1, :], tile("wvd_s1", [P, N], U8)]
 
         def quantize(a):
-            grouped = tile(f"grouped{a}", [P, N, PACK], BF16)
-            for copy, n0, n1 in ((nc.scalar.copy, 0, SPLIT), (nc.vector.tensor_copy, SPLIT, N)):
-                copy(
-                    out=grouped[:, n0:n1, :].rearrange("p (c i) t -> p c t i", i=4),
-                    in_=wvd_raw[a][:, :, n0:n1].rearrange("p t (c i) -> p c t i", i=4),
+            grouped = [tile(f"grouped{a}{h}", [P, P, PACK], BF16) for h in range(HALVES)]
+            for h in range(HALVES):
+                nc.vector.tensor_copy(
+                    out=grouped[h][:].rearrange("p (c i) t -> p c t i", i=4),
+                    in_=wvd_raw[a][:, :, h * P : (h + 1) * P].rearrange("p t (c i) -> p c t i", i=4),
                 )
-            nc.vector.quantize_mx(
-                out=wvd_w[a][:].bitcast(FP8X4),
-                scales=wvd_s[a][:, :],
-                in_=grouped[:].rearrange("p n t -> p (n t)"),
-            )
+            for h in range(HALVES):
+                nc.vector.quantize_mx(
+                    out=wvd_w[a][:, h * P : (h + 1) * P].bitcast(FP8X4),
+                    scales=wvd_s[a][:, h * P : (h + 1) * P],
+                    in_=grouped[h][:].rearrange("p n t -> p (n t)"),
+                )
 
         ke = [psum.tile([P, J], F32, name=f"ke{h}") for h in range(HALVES)]
         ve = [psum.tile([P, J], F32, name=f"ve{h}") for h in range(HALVES)]

@@ -37,9 +37,9 @@ def tile_list_engram_dl_sigL_kernel(
         def tile(name, shape, dtype):
             return pool.tile(shape, dtype, name=name, align_bytes=64)
 
-        def load_scale_rows(plane, scales):
+        def load_scale_rows(plane, scales, which):
             rows = scales.rearrange("a (q r) n -> r q a n", r=4)
-            for r in range(4):
+            for r in which:
                 nc.sync.dma_start(out=plane[r:P:32, :, :].bitcast(I32), in_=rows[r].bitcast(I32))
 
         offsets = pool.tile([P, J // 16], U16, name="offsets")
@@ -85,15 +85,17 @@ def tile_list_engram_dl_sigL_kernel(
         load_words(wv4_w, wv4_words)
         load_table_scales()
         load_table(0)
+        load_scale_rows(wk_s, wk_scales, range(1))
         load_wvd(0)
-        load_scale_rows(wk_s, wk_scales)
+        load_scale_rows(wk_s, wk_scales, range(1, 4))
         load_table(1)
+        load_scale_rows(wv4_s, wv4_scales, range(1))
         load_wvd(1)
 
         nc.vector.tensor_copy(got_s[0][:], tab_s[:].indirect(offsets[:]))
         nc.sync.dma_start(out=got_s[1][0:112, :].bitcast(I32), in_=got_s[0][16:P, :].bitcast(I32))
-        load_scale_rows(wv4_s, wv4_scales)
         load_rows(st_sb, st, 0)
+        load_scale_rows(wv4_s, wv4_scales, range(1, 4))
         load_rows(st_sb, st, 1)
         load_rows(r_sb, rT, 0)
         load_rows(r_sb, rT, 1)

@@ -82,20 +82,21 @@ def tile_list_engram_dl_sigL_kernel(
 
         nc.sync.dma_start(offsets[:], offs)
         load_words(wk_w, wk_words)
-        load_words(wv4_w, wv4_words)
         load_table_scales()
         load_table(0)
-        load_scale_rows(wk_s, wk_scales, range(1))
+        load_scale_rows(wk_s, wk_scales, range(2))
         load_wvd(0)
-        load_scale_rows(wk_s, wk_scales, range(1, 4))
+        load_scale_rows(wk_s, wk_scales, range(2, 4))
         load_table(1)
-        load_scale_rows(wv4_s, wv4_scales, range(1))
+        load_scale_rows(wv4_s, wv4_scales, range(2))
         load_wvd(1)
 
         nc.vector.tensor_copy(got_s[0][:], tab_s[:].indirect(offsets[:]))
         nc.sync.dma_start(out=got_s[1][0:112, :].bitcast(I32), in_=got_s[0][16:P, :].bitcast(I32))
+        load_words(wv4_w, wv4_words)
+        load_scale_rows(wv4_s, wv4_scales, range(2, 3))
         load_rows(st_sb, st, 0)
-        load_scale_rows(wv4_s, wv4_scales, range(1, 4))
+        load_scale_rows(wv4_s, wv4_scales, range(3, 4))
         load_rows(st_sb, st, 1)
         load_rows(r_sb, rT, 0)
         load_rows(r_sb, rT, 1)

@@ -87,16 +87,16 @@ def tile_list_engram_dl_sigL_kernel(
         load_scale_rows(wk_s, wk_scales, range(2))
         load_wvd(0)
         load_scale_rows(wk_s, wk_scales, range(2, 4))
+        load_scale_rows(wv4_s, wv4_scales, range(1))
         load_table(1)
-        load_scale_rows(wv4_s, wv4_scales, range(2))
+        load_scale_rows(wv4_s, wv4_scales, range(1, 2))
         load_wvd(1)
 
         nc.vector.tensor_copy(got_s[0][:], tab_s[:].indirect(offsets[:]))
         nc.sync.dma_start(out=got_s[1][0:112, :].bitcast(I32), in_=got_s[0][16:P, :].bitcast(I32))
         load_words(wv4_w, wv4_words)
-        load_scale_rows(wv4_s, wv4_scales, range(2, 3))
+        load_scale_rows(wv4_s, wv4_scales, range(2, 4))
         load_rows(st_sb, st, 0)
-        load_scale_rows(wv4_s, wv4_scales, range(3, 4))
         load_rows(st_sb, st, 1)
         load_rows(r_sb, rT, 0)
         load_rows(r_sb, rT, 1)

@@ -23,7 +23,10 @@ K_PASS = P * PACK
 PASSES = K // K_PASS
 HALVES = N // P
 QUADS = 4
+QUAD = P // QUADS
+ROWS = 4
 LAST = 128
+COMPACT = P - QUAD
 
 
 def tile_list_engram_dl_sigL_kernel(
@@ -37,11 +40,6 @@ def tile_list_engram_dl_sigL_kernel(
         def tile(name, shape, dtype):
             return pool.tile(shape, dtype, name=name, align_bytes=64)
 
-        def load_scale_rows(plane, scales, which):
-            rows = scales.rearrange("a (q r) n -> r q a n", r=4)
-            for r in which:
-                nc.sync.dma_start(out=plane[r:P:32, :, :].bitcast(I32), in_=rows[r].bitcast(I32))
-
         offsets = pool.tile([P, J // 16], U16, name="offsets")
         tab_w = [tile(f"tab_w{a}", [P, T], U32) for a in range(PASSES)]
         tab_s = tile("tab_s", [P, T], U8)
@@ -53,17 +51,18 @@ def tile_list_engram_dl_sigL_kernel(
         st_sb = [tile(f"st{h}", [P, J], F32) for h in range(HALVES)]
         r_sb = [tile(f"r{h}", [P, T], F32) for h in range(HALVES)]
         got_w = [tile(f"got_w{a}", [P, J], U32) for a in range(PASSES)]
-        got_s = [tile(f"got_s{a}", [P, J], U8) for a in range(PASSES)]
+        got_rows = tile("got_rows", [P, J], U8)
+        got_s = tile("got_s", [P, PASSES, J], U8)
 
-        nc.vector.memset(tab_s[:].bitcast(I32), 0)
-        for plane in (wk_s, wv4_s):
-            nc.vector.memset(plane[:].rearrange("p a n -> p (a n)").bitcast(I32), 0)
-        nc.vector.memset(got_s[1][:].bitcast(I32), 0)
+        nc.vector.memset(wk_s[:].rearrange("p a n -> p (a n)").bitcast(I32), 0)
+        nc.vector.memset(tab_s[0:COMPACT, :].bitcast(I32), 0)
+        nc.vector.memset(got_s[:].rearrange("p a j -> p (a j)").bitcast(I32), 0)
+        nc.vector.memset(wv4_s[:].rearrange("p a n -> p (a n)").bitcast(I32), 0)
 
-        def load_table_scales():
-            rows = tab_scales.rearrange("a (q r) t -> r q a t", r=4)
-            for r in range(4):
-                nc.sync.dma_start(out=tab_s[r:P:16, :].bitcast(I32), in_=rows[r].bitcast(I32))
+        def load_scale_rows(plane, scales, which):
+            rows = scales.rearrange("a (q r) n -> r q a n", r=ROWS)
+            for r in which:
+                nc.sync.dma_start(out=plane[r:P:QUAD, :, :].bitcast(I32), in_=rows[r].bitcast(I32))
 
         def load_words(dst, words):
             nc.sync.dma_start(out=dst[:].bitcast(I32), in_=words.rearrange("a p b -> p a b").bitcast(I32))
@@ -81,101 +80,122 @@ def tile_list_engram_dl_sigL_kernel(
             nc.sync.dma_start(out=tiles[h][:], in_=src[h * P : (h + 1) * P, :])
 
         nc.sync.dma_start(offsets[:], offs)
-        load_words(wk_w, wk_words)
-        load_table_scales()
+        nc.sync.dma_start(
+            out=tab_s[COMPACT:P, :].bitcast(I32), in_=tab_scales.rearrange("a q t -> q a t").bitcast(I32)
+        )
         load_table(0)
-        load_scale_rows(wk_s, wk_scales, range(2))
+        load_scale_rows(wk_s, wk_scales, range(ROWS))
         load_wvd(0)
-        load_scale_rows(wk_s, wk_scales, range(2, 4))
-        load_scale_rows(wv4_s, wv4_scales, range(1))
         load_table(1)
-        load_scale_rows(wv4_s, wv4_scales, range(1, 2))
-        load_wvd(1)
+        load_scale_rows(wv4_s, wv4_scales, range(1))
 
-        nc.vector.tensor_copy(got_s[0][:], tab_s[:].indirect(offsets[:]))
-        nc.sync.dma_start(out=got_s[1][0:112, :].bitcast(I32), in_=got_s[0][16:P, :].bitcast(I32))
-        load_words(wv4_w, wv4_words)
-        load_scale_rows(wv4_s, wv4_scales, range(2, 4))
+        nc.vector.tensor_copy(got_rows[:], tab_s[:].indirect(offsets[:]))
+        span = ROWS * PASSES
+        for q in range(QUADS):
+            nc.sync.dma_start(
+                out=got_s[q * QUAD : q * QUAD + ROWS, :, :].bitcast(I32),
+                in_=got_rows[COMPACT + q * span : COMPACT + (q + 1) * span, :].bitcast(I32),
+            )
+        load_words(wk_w, wk_words)
+        load_wvd(1)
         load_rows(st_sb, st, 0)
+        load_words(wv4_w, wv4_words)
+        load_scale_rows(wv4_s, wv4_scales, range(1, ROWS))
         load_rows(st_sb, st, 1)
         load_rows(r_sb, rT, 0)
         load_rows(r_sb, rT, 1)
 
         wvd_w = [tile(f"wvd_w{a}", [P, N], U32) for a in range(PASSES)]
-        wvd_s = [wk_s[4:P, 1, :], tile("wvd_s1", [P, N], U8)]
+        wvd_s = [tile(f"wvd_s{a}", [P, N], U8) for a in range(PASSES)]
+        grouped = [[tile(f"grouped{a}{h}", [P, P, PACK], BF16) for h in range(HALVES)] for a in range(PASSES)]
 
-        def quantize(a):
-            grouped = [tile(f"grouped{a}{h}", [P, P, PACK], BF16) for h in range(HALVES)]
-            for h in range(HALVES):
-                nc.vector.tensor_copy(
-                    out=grouped[h][:].rearrange("p (c i) t -> p c t i", i=4),
-                    in_=wvd_raw[a][:, :, h * P : (h + 1) * P].rearrange("p t (c i) -> p c t i", i=4),
-                )
-            for h in range(HALVES):
-                nc.vector.quantize_mx(
-                    out=wvd_w[a][:, h * P : (h + 1) * P].bitcast(FP8X4),
-                    scales=wvd_s[a][:, h * P : (h + 1) * P],
-                    in_=grouped[h][:].rearrange("p n t -> p (n t)"),
-                )
+        def interleave(copy, a, h):
+            copy(
+                out=grouped[a][h][:].rearrange("p (c i) t -> p c t i", i=4),
+                in_=wvd_raw[a][:, :, h * P : (h + 1) * P].rearrange("p t (c i) -> p c t i", i=4),
+            )
+
+        def quantize(a, h):
+            nc.vector.quantize_mx(
+                out=wvd_w[a][:, h * P : (h + 1) * P].bitcast(FP8X4),
+                scales=wvd_s[a][:, h * P : (h + 1) * P],
+                in_=grouped[a][h][:].rearrange("p n t -> p (n t)"),
+            )
 
         ke = [psum.tile([P, J], F32, name=f"ke{h}") for h in range(HALVES)]
-        ve = [psum.tile([P, J], F32, name=f"ve{h}") for h in range(HALVES)]
+        halves = [slice(c * J // 2, (c + 1) * J // 2) for c in range(2)]
+        whole = slice(0, J)
+        ve0 = [psum.tile([P, J // 2], F32, name=f"ve0{c}") for c in range(2)]
+        ve1 = psum.tile([P, J], F32, name="ve1")
 
-        def fp4_pass(acc, words, scales, a, h, start, stop):
+        def mx_pass(acc, cols, lhsT, lhsT_scale, a, start, stop):
             nc.tensor.matmul_mx(
                 out=acc[:],
-                lhsT=words[:, a, 2 * h * P : 2 * (h + 1) * P].bitcast(FP4X4),
-                lhsT_scale=scales[:, a, h * P : (h + 1) * P],
-                rhs=got_w[a][:].bitcast(FP8X4),
-                rhs_scale=got_s[a][:],
+                lhsT=lhsT,
+                lhsT_scale=lhsT_scale,
+                rhs=got_w[a][:, cols].bitcast(FP8X4),
+                rhs_scale=got_s[:, a, cols],
                 start=start,
                 stop=stop,
             )
 
-        def fp8_pass(a, h, start, stop):
-            nc.tensor.matmul_mx(
-                out=ve[h][:],
-                lhsT=wvd_w[a][:, h * P : (h + 1) * P].bitcast(FP8X4),
-                lhsT_scale=wvd_s[a][:, h * P : (h + 1) * P],
-                rhs=got_w[a][:].bitcast(FP8X4),
-                rhs_scale=got_s[a][:],
-                start=start,
-                stop=stop,
-            )
+        def fp4_pass(acc, cols, words, scales, a, h, start, stop):
+            codes = words[:, a, 2 * h * P : 2 * (h + 1) * P].bitcast(FP4X4)
+            mx_pass(acc, cols, codes, scales[:, a, h * P : (h + 1) * P], a, start, stop)
 
-        nc.vector.tensor_copy(got_w[0][:], tab_w[0][:].indirect(offsets[:]))
-        for h in range(HALVES):
-            fp4_pass(ke[h], wk_w, wk_s, 0, h, True, False)
-        quantize(0)
-        for h in range(HALVES):
-            fp8_pass(0, h, True, False)
-        nc.vector.tensor_copy(got_w[1][:], tab_w[1][:].indirect(offsets[:]))
-        for h in range(HALVES):
-            fp4_pass(ke[h], wk_w, wk_s, 1, h, False, True)
-        quantize(1)
+        def fp8_pass(acc, cols, a, h, start, stop):
+            chans = slice(h * P, (h + 1) * P)
+            mx_pass(acc, cols, wvd_w[a][:, chans].bitcast(FP8X4), wvd_s[a][:, chans], a, start, stop)
 
         gate = [tile(f"gate{h}", [P, J], F32) for h in range(HALVES)]
 
         def make_gate(h):
-            pieces = 2 - h
-            for c in range(pieces):
-                cols = slice(c * J // pieces, (c + 1) * J // pieces)
-                logit = tile(f"logit{h}{c}", [P, J // pieces], F32)
+            for c in range(2):
+                cols = slice(c * J // 2, (c + 1) * J // 2)
+                logit = tile(f"logit{h}{c}", [P, J // 2], F32)
                 nc.vector.tensor_tensor(logit[:], ke[h][:, cols], st_sb[h][:, cols], MULT)
                 nc.scalar.activation(gate[h][:, cols], logit[:], SIGMOID)
 
+        nc.vector.tensor_copy(got_w[0][:], tab_w[0][:].indirect(offsets[:]))
         for h in range(HALVES):
-            make_gate(h)
+            interleave(nc.vector.tensor_copy, 0, h)
+        for h in range(HALVES):
+            quantize(0, h)
+        nc.vector.tensor_copy(got_w[1][:], tab_w[1][:].indirect(offsets[:]))
+        unread = psum.tile([P, J], F32, name="unread")
+        nc.tensor.matmul_mx(
+            out=unread[:],
+            lhsT=wvd_w[0][:, 0:P].bitcast(FP8X4),
+            lhsT_scale=wvd_s[0][:, 0:P],
+            rhs=got_w[0][:].bitcast(FP8X4),
+            rhs_scale=got_rows[:],
+            start=True,
+            stop=True,
+        )
         for h in range(HALVES):
             for a in range(PASSES):
-                fp4_pass(ve[h], wv4_w, wv4_s, a, h, False, False)
-            fp8_pass(1, h, False, True)
+                fp4_pass(ke[h], whole, wk_w, wk_s, a, h, a == 0, a == PASSES - 1)
+        for h in range(HALVES):
+            interleave(nc.vector.tensor_copy, 1, h)
+        for h in range(HALVES):
+            quantize(1, h)
+        for h in range(HALVES):
+            make_gate(h)
+        for c, cols in enumerate(halves):
+            for a in range(PASSES):
+                fp8_pass(ve0[c], cols, a, 0, a == 0, False)
+            for a in range(PASSES):
+                fp4_pass(ve0[c], cols, wv4_w, wv4_s, a, 0, False, a == PASSES - 1)
+        for a in range(PASSES):
+            fp4_pass(ve1, whole, wv4_w, wv4_s, a, 1, a == 0, False)
+        for a in range(PASSES):
+            fp8_pass(ve1, whole, a, 1, False, a == PASSES - 1)
+        ve = [[ve0[c][:] for c in range(2)], [ve1[:, cols] for cols in halves]]
 
-        gated = tile("gated", [P, J], F32)
+        gated = st_sb[1]
         for h, cuts in enumerate(((0, J // 2, J), (0, J // 2, J - LAST, J))):
-            for c in range(2):
-                cols = slice(c * J // 2, (c + 1) * J // 2)
-                nc.vector.tensor_tensor(gated[:, cols], ve[h][:, cols], gate[h][:, cols], MULT)
+            for c, cols in enumerate(halves):
+                nc.vector.tensor_tensor(gated[:, cols], ve[h][c], gate[h][:, cols], MULT)
             for j0, j1 in zip(cuts, cuts[1:]):
                 res = tile(f"res{h}_{j0}", [P, j1 - j0], F32)
                 nc.vector.tensor_tensor(

@@ -45,7 +45,7 @@ def tile_list_engram_dl_sigL_kernel(
         tab_s = tile("tab_s", [P, T], U8)
         wk_w = tile("wk_w", [P, PASSES, 2 * N], U8)
         wk_s = tile("wk_s", [P, PASSES, N], U8)
-        wv4_w = tile("wv4_w", [P, PASSES, 2 * N], U8)
+        wv4_w = [tile(f"wv4_w{h}", [P, PASSES, 2 * P], U8) for h in range(HALVES)]
         wv4_s = tile("wv4_s", [P, PASSES, N], U8)
         wvd_raw = [tile(f"wvd_raw{a}", [P, PACK, N], F32) for a in range(PASSES)]
         st_sb = [tile(f"st{h}", [P, J], F32) for h in range(HALVES)]
@@ -59,6 +59,10 @@ def tile_list_engram_dl_sigL_kernel(
         nc.vector.memset(got_s[:].rearrange("p a j -> p (a j)").bitcast(I32), 0)
         nc.vector.memset(wv4_s[:].rearrange("p a n -> p (a n)").bitcast(I32), 0)
 
+        warm = tile("warm", [P, 1], F32)
+        nc.vector.memset(warm[:], 0.0)
+        nc.scalar.activation(warm[:], warm[:], SIGMOID)
+
         def load_scale_rows(plane, scales, which):
             rows = scales.rearrange("a (q r) n -> r q a n", r=ROWS)
             for r in which:
@@ -66,6 +70,10 @@ def tile_list_engram_dl_sigL_kernel(
 
         def load_words(dst, words):
             nc.sync.dma_start(out=dst[:].bitcast(I32), in_=words.rearrange("a p b -> p a b").bitcast(I32))
+
+        def load_wv4_words(h):
+            words = wv4_words[:, :, 2 * h * P : 2 * (h + 1) * P].rearrange("a p b -> p a b")
+            nc.sync.dma_start(out=wv4_w[h][:].bitcast(I32), in_=words.bitcast(I32))
 
         def load_table(a):
             nc.sync.dma_start(
@@ -99,10 +107,11 @@ def tile_list_engram_dl_sigL_kernel(
         load_words(wk_w, wk_words)
         load_wvd(1)
         load_rows(st_sb, st, 0)
-        load_words(wv4_w, wv4_words)
+        load_wv4_words(0)
         load_scale_rows(wv4_s, wv4_scales, range(1, ROWS))
         load_rows(st_sb, st, 1)
         load_rows(r_sb, rT, 0)
+        load_wv4_words(1)
         load_rows(r_sb, rT, 1)
 
         wvd_w = [tile(f"wvd_w{a}", [P, N], U32) for a in range(PASSES)]
@@ -122,11 +131,12 @@ def tile_list_engram_dl_sigL_kernel(
                 in_=grouped[a][h][:].rearrange("p n t -> p (n t)"),
             )
 
-        ke = [psum.tile([P, J], F32, name=f"ke{h}") for h in range(HALVES)]
         halves = [slice(c * J // 2, (c + 1) * J // 2) for c in range(2)]
         whole = slice(0, J)
         ve0 = [psum.tile([P, J // 2], F32, name=f"ve0{c}") for c in range(2)]
-        ve1 = psum.tile([P, J], F32, name="ve1")
+        ke0 = psum.tile([P, J], F32, name="ke0")
+        ke1 = [psum.tile([P, J // 2], F32, name=f"ke1{c}", tag=f"half1{c}") for c in range(2)]
+        ke = [[ke0[:, cols] for cols in halves], [ke1[c][:] for c in range(2)]]
 
         def mx_pass(acc, cols, lhsT, lhsT_scale, a, start, stop):
             nc.tensor.matmul_mx(
@@ -139,9 +149,13 @@ def tile_list_engram_dl_sigL_kernel(
                 stop=stop,
             )
 
-        def fp4_pass(acc, cols, words, scales, a, h, start, stop):
-            codes = words[:, a, 2 * h * P : 2 * (h + 1) * P].bitcast(FP4X4)
-            mx_pass(acc, cols, codes, scales[:, a, h * P : (h + 1) * P], a, start, stop)
+        def wk_pass(acc, cols, a, h):
+            codes = wk_w[:, a, 2 * h * P : 2 * (h + 1) * P].bitcast(FP4X4)
+            mx_pass(acc, cols, codes, wk_s[:, a, h * P : (h + 1) * P], a, a == 0, a == PASSES - 1)
+
+        def wv4_pass(acc, cols, a, h):
+            codes = wv4_w[h][:, a, :].bitcast(FP4X4)
+            mx_pass(acc, cols, codes, wv4_s[:, a, h * P : (h + 1) * P], a, False, a == PASSES - 1)
 
         def fp8_pass(acc, cols, a, h, start, stop):
             chans = slice(h * P, (h + 1) * P)
@@ -153,7 +167,7 @@ def tile_list_engram_dl_sigL_kernel(
             for c in range(2):
                 cols = slice(c * J // 2, (c + 1) * J // 2)
                 logit = tile(f"logit{h}{c}", [P, J // 2], F32)
-                nc.vector.tensor_tensor(logit[:], ke[h][:, cols], st_sb[h][:, cols], MULT)
+                nc.vector.tensor_tensor(logit[:], ke[h][c], st_sb[h][:, cols], MULT)
                 nc.scalar.activation(gate[h][:, cols], logit[:], SIGMOID)
 
         nc.vector.tensor_copy(got_w[0][:], tab_w[0][:].indirect(offsets[:]))
@@ -172,25 +186,26 @@ def tile_list_engram_dl_sigL_kernel(
             start=True,
             stop=True,
         )
-        for h in range(HALVES):
-            for a in range(PASSES):
-                fp4_pass(ke[h], whole, wk_w, wk_s, a, h, a == 0, a == PASSES - 1)
-        for h in range(HALVES):
-            interleave(nc.vector.tensor_copy, 1, h)
-        for h in range(HALVES):
-            quantize(1, h)
-        for h in range(HALVES):
-            make_gate(h)
+        for a in range(PASSES):
+            wk_pass(ke0, whole, a, 0)
         for c, cols in enumerate(halves):
             for a in range(PASSES):
-                fp8_pass(ve0[c], cols, a, 0, a == 0, False)
-            for a in range(PASSES):
-                fp4_pass(ve0[c], cols, wv4_w, wv4_s, a, 0, False, a == PASSES - 1)
-        for a in range(PASSES):
-            fp4_pass(ve1, whole, wv4_w, wv4_s, a, 1, a == 0, False)
-        for a in range(PASSES):
-            fp8_pass(ve1, whole, a, 1, False, a == PASSES - 1)
-        ve = [[ve0[c][:] for c in range(2)], [ve1[:, cols] for cols in halves]]
+                wk_pass(ke1[c], cols, a, 1)
+        interleave(nc.vector.tensor_copy, 1, 0)
+        interleave(nc.scalar.copy, 1, 1)
+        quantize(1, 0)
+        make_gate(0)
+        quantize(1, 1)
+        make_gate(1)
+        ve1 = [psum.tile([P, J // 2], F32, name=f"ve1{c}", tag=f"half1{c}") for c in range(2)]
+        for h, banks in enumerate((ve0, ve1)):
+            for c, cols in enumerate(halves):
+                order = range(PASSES) if (h, c) == (0, 0) else reversed(range(PASSES))
+                for i, a in enumerate(order):
+                    fp8_pass(banks[c], cols, a, h, i == 0, False)
+                for a in range(PASSES):
+                    wv4_pass(banks[c], cols, a, h)
+        ve = [[bank[:] for bank in banks] for banks in (ve0, ve1)]
 
         gated = st_sb[1]
         for h, cuts in enumerate(((0, J // 2, J), (0, J // 2, J - LAST, J))):

@@ -133,10 +133,10 @@ def tile_list_engram_dl_sigL_kernel(
 
         halves = [slice(c * J // 2, (c + 1) * J // 2) for c in range(2)]
         whole = slice(0, J)
-        ve0 = [psum.tile([P, J // 2], F32, name=f"ve0{c}") for c in range(2)]
+        ve0 = [psum.tile([P, J // 2], F32, name=f"ve0{c}", tag=f"ve0{c}") for c in range(2)]
         ke0 = psum.tile([P, J], F32, name="ke0")
-        ke1 = [psum.tile([P, J // 2], F32, name=f"ke1{c}", tag=f"half1{c}") for c in range(2)]
-        ke = [[ke0[:, cols] for cols in halves], [ke1[c][:] for c in range(2)]]
+        ke1 = psum.tile([P, J], F32, name="ke1", tag="ke1")
+        ke = [[bank[:, cols] for cols in halves] for bank in (ke0, ke1)]
 
         def mx_pass(acc, cols, lhsT, lhsT_scale, a, start, stop):
             nc.tensor.matmul_mx(
@@ -153,9 +153,9 @@ def tile_list_engram_dl_sigL_kernel(
             codes = wk_w[:, a, 2 * h * P : 2 * (h + 1) * P].bitcast(FP4X4)
             mx_pass(acc, cols, codes, wk_s[:, a, h * P : (h + 1) * P], a, a == 0, a == PASSES - 1)
 
-        def wv4_pass(acc, cols, a, h):
+        def wv4_pass(acc, cols, a, h, stop):
             codes = wv4_w[h][:, a, :].bitcast(FP4X4)
-            mx_pass(acc, cols, codes, wv4_s[:, a, h * P : (h + 1) * P], a, False, a == PASSES - 1)
+            mx_pass(acc, cols, codes, wv4_s[:, a, h * P : (h + 1) * P], a, False, stop)
 
         def fp8_pass(acc, cols, a, h, start, stop):
             chans = slice(h * P, (h + 1) * P)
@@ -176,41 +176,46 @@ def tile_list_engram_dl_sigL_kernel(
         for h in range(HALVES):
             quantize(0, h)
         nc.vector.tensor_copy(got_w[1][:], tab_w[1][:].indirect(offsets[:]))
-        unread = psum.tile([P, J], F32, name="unread")
-        nc.tensor.matmul_mx(
-            out=unread[:],
-            lhsT=wvd_w[0][:, 0:P].bitcast(FP8X4),
-            lhsT_scale=wvd_s[0][:, 0:P],
-            rhs=got_w[0][:].bitcast(FP8X4),
-            rhs_scale=got_rows[:],
-            start=True,
-            stop=True,
-        )
+        for width in (J, 64):
+            unread = psum.tile([P, width], F32, name=f"unread{width}")
+            nc.tensor.matmul_mx(
+                out=unread[:],
+                lhsT=wvd_w[0][:, 0:P].bitcast(FP8X4),
+                lhsT_scale=wvd_s[0][:, 0:P],
+                rhs=got_w[0][:, 0:width].bitcast(FP8X4),
+                rhs_scale=got_rows[:, 0:width],
+                start=True,
+                stop=True,
+            )
         for a in range(PASSES):
             wk_pass(ke0, whole, a, 0)
-        for c, cols in enumerate(halves):
-            for a in range(PASSES):
-                wk_pass(ke1[c], cols, a, 1)
+        for a in range(PASSES):
+            wk_pass(ke1, whole, a, 1)
         interleave(nc.vector.tensor_copy, 1, 0)
         interleave(nc.scalar.copy, 1, 1)
         quantize(1, 0)
         make_gate(0)
         quantize(1, 1)
         make_gate(1)
-        ve1 = [psum.tile([P, J // 2], F32, name=f"ve1{c}", tag=f"half1{c}") for c in range(2)]
-        for h, banks in enumerate((ve0, ve1)):
-            for c, cols in enumerate(halves):
-                order = range(PASSES) if (h, c) == (0, 0) else reversed(range(PASSES))
-                for i, a in enumerate(order):
-                    fp8_pass(banks[c], cols, a, h, i == 0, False)
-                for a in range(PASSES):
-                    wv4_pass(banks[c], cols, a, h)
-        ve = [[bank[:] for bank in banks] for banks in (ve0, ve1)]
+        def ve_group(bank, cols, h, wvd_last):
+            fp8_pass(bank, cols, 0, h, True, False)
+            if not wvd_last:
+                fp8_pass(bank, cols, 1, h, False, False)
+            for a in range(PASSES):
+                wv4_pass(bank, cols, a, h, a == PASSES - 1 and not wvd_last)
+            if wvd_last:
+                fp8_pass(bank, cols, 1, h, False, True)
 
         gated = st_sb[1]
         for h, cuts in enumerate(((0, J // 2, J), (0, J // 2, J - LAST, J))):
+            if h == 0:
+                banks = ve0
+            else:
+                banks = [psum.tile([P, J // 2], F32, name=f"ve1{c}", tag=tag) for c, tag in enumerate(("ke1", "ve00"))]
             for c, cols in enumerate(halves):
-                nc.vector.tensor_tensor(gated[:, cols], ve[h][c], gate[h][:, cols], MULT)
+                ve_group(banks[c], cols, h, (h, c) == (0, 1))
+            for c, cols in enumerate(halves):
+                nc.vector.tensor_tensor(gated[:, cols], banks[c][:], gate[h][:, cols], MULT)
             for j0, j1 in zip(cuts, cuts[1:]):
                 res = tile(f"res{h}_{j0}", [P, j1 - j0], F32)
                 nc.vector.tensor_tensor(

@@ -26,6 +26,7 @@ QUADS = 4
 QUAD = P // QUADS
 ROWS = 4
 LAST = 128
+NARROW = 32
 COMPACT = P - QUAD
 
 
@@ -116,19 +117,21 @@ def tile_list_engram_dl_sigL_kernel(
 
         wvd_w = [tile(f"wvd_w{a}", [P, N], U32) for a in range(PASSES)]
         wvd_s = [tile(f"wvd_s{a}", [P, N], U8) for a in range(PASSES)]
-        grouped = [[tile(f"grouped{a}{h}", [P, P, PACK], BF16) for h in range(HALVES)] for a in range(PASSES)]
+        grouped = {}
 
-        def interleave(copy, a, h):
+        def interleave(copy, a, n0, n1):
+            piece = tile(f"grouped{a}_{n0}", [P, n1 - n0, PACK], BF16)
+            grouped.setdefault((a, n0), piece)
             copy(
-                out=grouped[a][h][:].rearrange("p (c i) t -> p c t i", i=4),
-                in_=wvd_raw[a][:, :, h * P : (h + 1) * P].rearrange("p t (c i) -> p c t i", i=4),
+                out=piece[:].rearrange("p (c i) t -> p c t i", i=4),
+                in_=wvd_raw[a][:, :, n0:n1].rearrange("p t (c i) -> p c t i", i=4),
             )
 
-        def quantize(a, h):
+        def quantize(a, n0, n1):
             nc.vector.quantize_mx(
-                out=wvd_w[a][:, h * P : (h + 1) * P].bitcast(FP8X4),
-                scales=wvd_s[a][:, h * P : (h + 1) * P],
-                in_=grouped[a][h][:].rearrange("p n t -> p (n t)"),
+                out=wvd_w[a][:, n0:n1].bitcast(FP8X4),
+                scales=wvd_s[a][:, n0:n1],
+                in_=grouped[a, n0][:].rearrange("p n t -> p (n t)"),
             )
 
         halves = [slice(c * J // 2, (c + 1) * J // 2) for c in range(2)]
@@ -171,19 +174,22 @@ def tile_list_engram_dl_sigL_kernel(
                 nc.scalar.activation(gate[h][:, cols], logit[:], SIGMOID)
 
         nc.vector.tensor_copy(got_w[0][:], tab_w[0][:].indirect(offsets[:]))
-        for h in range(HALVES):
-            interleave(nc.vector.tensor_copy, 0, h)
-        for h in range(HALVES):
-            quantize(0, h)
+        quarters = ((0, P // 2), (P // 2, P))
+        for n0, n1 in quarters:
+            interleave(nc.vector.tensor_copy, 0, n0, n1)
+        for n0, n1 in quarters:
+            quantize(0, n0, n1)
+        interleave(nc.vector.tensor_copy, 0, P, N)
+        quantize(0, P, N)
         nc.vector.tensor_copy(got_w[1][:], tab_w[1][:].indirect(offsets[:]))
-        for width in (J, 64):
-            unread = psum.tile([P, width], F32, name=f"unread{width}")
+        for i in range(2):
+            unread = psum.tile([NARROW, J], F32, name=f"unread{i}")
             nc.tensor.matmul_mx(
                 out=unread[:],
-                lhsT=wvd_w[0][:, 0:P].bitcast(FP8X4),
-                lhsT_scale=wvd_s[0][:, 0:P],
-                rhs=got_w[0][:, 0:width].bitcast(FP8X4),
-                rhs_scale=got_rows[:, 0:width],
+                lhsT=wvd_w[0][:, 0:NARROW].bitcast(FP8X4),
+                lhsT_scale=wvd_s[0][:, 0:NARROW],
+                rhs=got_w[0][:].bitcast(FP8X4),
+                rhs_scale=got_rows[:],
                 start=True,
                 stop=True,
             )
@@ -191,11 +197,11 @@ def tile_list_engram_dl_sigL_kernel(
             wk_pass(ke0, whole, a, 0)
         for a in range(PASSES):
             wk_pass(ke1, whole, a, 1)
-        interleave(nc.vector.tensor_copy, 1, 0)
-        interleave(nc.scalar.copy, 1, 1)
-        quantize(1, 0)
+        interleave(nc.vector.tensor_copy, 1, 0, P)
+        interleave(nc.scalar.copy, 1, P, N)
+        quantize(1, 0, P)
         make_gate(0)
-        quantize(1, 1)
+        quantize(1, P, N)
         make_gate(1)
         def ve_group(bank, cols, h, wvd_last):
             fp8_pass(bank, cols, 0, h, True, False)

@@ -27,6 +27,7 @@ QUAD = P // QUADS
 ROWS = 4
 LAST = 128
 NARROW = 32
+FIRST = 128
 COMPACT = P - QUAD
 
 
@@ -92,9 +93,9 @@ def tile_list_engram_dl_sigL_kernel(
         nc.sync.dma_start(
             out=tab_s[COMPACT:P, :].bitcast(I32), in_=tab_scales.rearrange("a q t -> q a t").bitcast(I32)
         )
-        load_table(0)
-        load_scale_rows(wk_s, wk_scales, range(ROWS))
         load_wvd(0)
+        load_scale_rows(wk_s, wk_scales, range(ROWS))
+        load_table(0)
         load_table(1)
         load_scale_rows(wv4_s, wv4_scales, range(1))
 
@@ -115,8 +116,12 @@ def tile_list_engram_dl_sigL_kernel(
         load_wv4_words(1)
         load_rows(r_sb, rT, 1)
 
-        wvd_w = [tile(f"wvd_w{a}", [P, N], U32) for a in range(PASSES)]
-        wvd_s = [tile(f"wvd_s{a}", [P, N], U8) for a in range(PASSES)]
+        wvd_w_all = tile("wvd_w", [P, PASSES * N], U32)
+        wvd_s_all = tile("wvd_s", [P, PASSES * N], U8)
+        wvd_w = [wvd_w_all[:, a * N : (a + 1) * N] for a in range(PASSES)]
+        wvd_s = [wvd_s_all[:, a * N : (a + 1) * N] for a in range(PASSES)]
+        nc.vector.memset(wvd_w[1].bitcast(I32), 0)
+        nc.vector.memset(wvd_s[1].bitcast(I32), 0)
         grouped = {}
 
         def interleave(copy, a, n0, n1):
@@ -173,23 +178,21 @@ def tile_list_engram_dl_sigL_kernel(
                 nc.vector.tensor_tensor(logit[:], ke[h][c], st_sb[h][:, cols], MULT)
                 nc.scalar.activation(gate[h][:, cols], logit[:], SIGMOID)
 
-        nc.vector.tensor_copy(got_w[0][:], tab_w[0][:].indirect(offsets[:]))
-        quarters = ((0, P // 2), (P // 2, P))
-        for n0, n1 in quarters:
-            interleave(nc.vector.tensor_copy, 0, n0, n1)
-        for n0, n1 in quarters:
-            quantize(0, n0, n1)
-        interleave(nc.vector.tensor_copy, 0, P, N)
-        quantize(0, P, N)
+        for h in range(HALVES):
+            interleave(nc.vector.tensor_copy, 0, h * P, (h + 1) * P)
+        for h in range(HALVES):
+            quantize(0, h * P, (h + 1) * P)
+        for j0, j1 in ((0, FIRST), (FIRST, J)):
+            nc.vector.tensor_copy(got_w[0][:, j0:j1], tab_w[0][:].indirect(offsets[:, j0 // 16 : j1 // 16]))
         nc.vector.tensor_copy(got_w[1][:], tab_w[1][:].indirect(offsets[:]))
         for i in range(2):
             unread = psum.tile([NARROW, J], F32, name=f"unread{i}")
             nc.tensor.matmul_mx(
                 out=unread[:],
-                lhsT=wvd_w[0][:, 0:NARROW].bitcast(FP8X4),
-                lhsT_scale=wvd_s[0][:, 0:NARROW],
-                rhs=got_w[0][:].bitcast(FP8X4),
-                rhs_scale=got_rows[:],
+                lhsT=got_w[0][:, 0:NARROW].bitcast(FP8X4),
+                lhsT_scale=got_rows[:, 0:NARROW],
+                rhs=wvd_w_all[:].bitcast(FP8X4),
+                rhs_scale=wvd_s_all[:],
                 start=True,
                 stop=True,
             )

@@ -61,10 +61,6 @@ def tile_list_engram_dl_sigL_kernel(
         nc.vector.memset(got_s[:].rearrange("p a j -> p (a j)").bitcast(I32), 0)
         nc.vector.memset(wv4_s[:].rearrange("p a n -> p (a n)").bitcast(I32), 0)
 
-        warm = tile("warm", [P, 1], F32)
-        nc.vector.memset(warm[:], 0.0)
-        nc.scalar.activation(warm[:], warm[:], SIGMOID)
-
         def load_scale_rows(plane, scales, which):
             rows = scales.rearrange("a (q r) n -> r q a n", r=ROWS)
             for r in which:
@@ -201,7 +197,7 @@ def tile_list_engram_dl_sigL_kernel(
         for a in range(PASSES):
             wk_pass(ke1, whole, a, 1)
         interleave(nc.vector.tensor_copy, 1, 0, P)
-        interleave(nc.scalar.copy, 1, P, N)
+        interleave(nc.vector.tensor_copy, 1, P, N)
         quantize(1, 0, P)
         make_gate(0)
         quantize(1, P, N)

@@ -40,7 +40,7 @@ def tile_list_engram_dl_sigL_kernel(
         psum = ctx.enter_context(tc.psum_pool(name="psum", bufs=1))
 
         def tile(name, shape, dtype):
-            return pool.tile(shape, dtype, name=name, align_bytes=64)
+            return pool.tile(shape, dtype, name=name, align_bytes=256)
 
         offsets = pool.tile([P, J // 16], U16, name="offsets")
         tab_w = [tile(f"tab_w{a}", [P, T], U32) for a in range(PASSES)]

@@ -97,7 +97,7 @@ def tile_list_engram_dl_sigL_kernel(
 
         nc.vector.tensor_copy(got_rows[:], tab_s[:].indirect(offsets[:]))
         span = ROWS * PASSES
-        for q in range(QUADS):
+        for q in (0, 2, 1, 3):
             nc.sync.dma_start(
                 out=got_s[q * QUAD : q * QUAD + ROWS, :, :].bitcast(I32),
                 in_=got_rows[COMPACT + q * span : COMPACT + (q + 1) * span, :].bitcast(I32),

@@ -27,7 +27,6 @@ QUAD = P // QUADS
 ROWS = 4
 LAST = 128
 NARROW = 32
-FIRST = 128
 COMPACT = P - QUAD
 
 
@@ -39,8 +38,8 @@ def tile_list_engram_dl_sigL_kernel(
         pool = ctx.enter_context(tc.tile_pool(name="pool", bufs=1))
         psum = ctx.enter_context(tc.psum_pool(name="psum", bufs=1))
 
-        def tile(name, shape, dtype):
-            return pool.tile(shape, dtype, name=name, align_bytes=256)
+        def tile(name, shape, dtype, tag=None):
+            return pool.tile(shape, dtype, name=name, tag=tag or name, align_bytes=256)
 
         offsets = pool.tile([P, J // 16], U16, name="offsets")
         tab_w = [tile(f"tab_w{a}", [P, T], U32) for a in range(PASSES)]
@@ -54,11 +53,9 @@ def tile_list_engram_dl_sigL_kernel(
         r_sb = [tile(f"r{h}", [P, T], F32) for h in range(HALVES)]
         got_w = [tile(f"got_w{a}", [P, J], U32) for a in range(PASSES)]
         got_rows = tile("got_rows", [P, J], U8)
-        got_s = tile("got_s", [P, PASSES, J], U8)
 
         nc.vector.memset(wk_s[:].rearrange("p a n -> p (a n)").bitcast(I32), 0)
         nc.vector.memset(tab_s[0:COMPACT, :].bitcast(I32), 0)
-        nc.vector.memset(got_s[:].rearrange("p a j -> p (a j)").bitcast(I32), 0)
         nc.vector.memset(wv4_s[:].rearrange("p a n -> p (a n)").bitcast(I32), 0)
 
         def load_scale_rows(plane, scales, which):
@@ -96,6 +93,7 @@ def tile_list_engram_dl_sigL_kernel(
         load_scale_rows(wv4_s, wv4_scales, range(1))
 
         nc.vector.tensor_copy(got_rows[:], tab_s[:].indirect(offsets[:]))
+        got_s = tile("got_s", [P, PASSES, J], U8, tag="tab_s")
         span = ROWS * PASSES
         for q in (0, 2, 1, 3):
             nc.sync.dma_start(
@@ -116,8 +114,6 @@ def tile_list_engram_dl_sigL_kernel(
         wvd_s_all = tile("wvd_s", [P, PASSES * N], U8)
         wvd_w = [wvd_w_all[:, a * N : (a + 1) * N] for a in range(PASSES)]
         wvd_s = [wvd_s_all[:, a * N : (a + 1) * N] for a in range(PASSES)]
-        nc.vector.memset(wvd_w[1].bitcast(I32), 0)
-        nc.vector.memset(wvd_s[1].bitcast(I32), 0)
         grouped = {}
 
         def interleave(copy, a, n0, n1):
@@ -178,17 +174,16 @@ def tile_list_engram_dl_sigL_kernel(
             interleave(nc.vector.tensor_copy, 0, h * P, (h + 1) * P)
         for h in range(HALVES):
             quantize(0, h * P, (h + 1) * P)
-        for j0, j1 in ((0, FIRST), (FIRST, J)):
-            nc.vector.tensor_copy(got_w[0][:, j0:j1], tab_w[0][:].indirect(offsets[:, j0 // 16 : j1 // 16]))
-        nc.vector.tensor_copy(got_w[1][:], tab_w[1][:].indirect(offsets[:]))
-        for i in range(2):
-            unread = psum.tile([NARROW, J], F32, name=f"unread{i}")
+        for a in range(PASSES):
+            nc.vector.tensor_copy(got_w[a][:], tab_w[a][:].indirect(offsets[:]))
+        unread = psum.tile([NARROW, J], F32, name="unread")
+        for i in range(3):
             nc.tensor.matmul_mx(
                 out=unread[:],
-                lhsT=got_w[0][:, 0:NARROW].bitcast(FP8X4),
-                lhsT_scale=got_rows[:, 0:NARROW],
-                rhs=wvd_w_all[:].bitcast(FP8X4),
-                rhs_scale=wvd_s_all[:],
+                lhsT=wvd_w[0][:, 0:NARROW].bitcast(FP8X4),
+                lhsT_scale=wvd_s[0][:, 0:NARROW],
+                rhs=tab_w[0][:, 0:J].bitcast(FP8X4),
+                rhs_scale=got_rows[:],
                 start=True,
                 stop=True,
             )

from contextlib import ExitStack

import concourse.mybir as mybir

K, N, T, J = 1024, 256, 1024, 512
FLOPS = 3 * 2 * K * N * J

F32 = mybir.dt.float32
BF16 = mybir.dt.bfloat16
I32 = mybir.dt.int32
U32 = mybir.dt.uint32
U16 = mybir.dt.uint16
U8 = mybir.dt.uint8
FP8X4 = mybir.dt.float8_e4m3fn_x4
FP4X4 = mybir.dt.float4_e2m1fn_x4
MULT = mybir.AluOpType.mult
ADD = mybir.AluOpType.add
SIGMOID = mybir.ActivationFunctionType.Sigmoid

P = 128
PACK = 4
K_PASS = P * PACK
PASSES = K // K_PASS
HALVES = N // P
QUADS = 4
QUAD = P // QUADS
ROWS = 4
LAST = 128
NARROW = 32
COMPACT = P - QUAD


def tile_list_engram_dl_sigL_kernel(
    tc, tab_words, tab_scales, wk_words, wk_scales, wv4_words, wv4_scales, wvd, st, rT, offs, out
):
    nc = tc.nc
    with ExitStack() as ctx:
        pool = ctx.enter_context(tc.tile_pool(name="pool", bufs=1))
        psum = ctx.enter_context(tc.psum_pool(name="psum", bufs=1))

        def tile(name, shape, dtype, tag=None):
            return pool.tile(shape, dtype, name=name, tag=tag or name, align_bytes=256)

        offsets = pool.tile([P, J // 16], U16, name="offsets")
        tab_w = [tile(f"tab_w{a}", [P, T], U32) for a in range(PASSES)]
        tab_s = tile("tab_s", [P, T], U8)
        wk_w = tile("wk_w", [P, PASSES, 2 * N], U8)
        wk_s = tile("wk_s", [P, PASSES, N], U8)
        wv4_w = [tile(f"wv4_w{h}", [P, PASSES, 2 * P], U8) for h in range(HALVES)]
        wv4_s = tile("wv4_s", [P, PASSES, N], U8)
        wvd_raw = [tile(f"wvd_raw{a}", [P, PACK, N], F32) for a in range(PASSES)]
        st_sb = [tile(f"st{h}", [P, J], F32) for h in range(HALVES)]
        r_sb = [tile(f"r{h}", [P, T], F32) for h in range(HALVES)]
        got_w = [tile(f"got_w{a}", [P, J], U32) for a in range(PASSES)]
        got_rows = tile("got_rows", [P, J], U8)

        nc.vector.memset(wk_s[:].rearrange("p a n -> p (a n)").bitcast(I32), 0)
        nc.vector.memset(tab_s[0:COMPACT, :].bitcast(I32), 0)
        nc.vector.memset(wv4_s[:].rearrange("p a n -> p (a n)").bitcast(I32), 0)

        def load_scale_rows(plane, scales, which):
            rows = scales.rearrange("a (q r) n -> r q a n", r=ROWS)
            for r in which:
                nc.sync.dma_start(out=plane[r:P:QUAD, :, :].bitcast(I32), in_=rows[r].bitcast(I32))

        def load_words(dst, words):
            nc.sync.dma_start(out=dst[:].bitcast(I32), in_=words.rearrange("a p b -> p a b").bitcast(I32))

        def load_wv4_words(h):
            words = wv4_words[:, :, 2 * h * P : 2 * (h + 1) * P].rearrange("a p b -> p a b")
            nc.sync.dma_start(out=wv4_w[h][:].bitcast(I32), in_=words.bitcast(I32))

        def load_table(a):
            nc.sync.dma_start(
                out=tab_w[a][:].bitcast(I32), in_=tab_words[a].rearrange("p t i -> p (t i)").bitcast(I32)
            )

        def load_wvd(a):
            rows = wvd[a * K_PASS : (a + 1) * K_PASS, :]
            nc.sync.dma_start(out=wvd_raw[a][:], in_=rows.rearrange("(p t) n -> p t n", t=PACK))

        def load_rows(tiles, src, h):
            nc.sync.dma_start(out=tiles[h][:], in_=src[h * P : (h + 1) * P, :])

        nc.sync.dma_start(offsets[:], offs)
        nc.sync.dma_start(
            out=tab_s[COMPACT:P, :].bitcast(I32), in_=tab_scales.rearrange("a q t -> q a t").bitcast(I32)
        )
        load_wvd(0)
        load_scale_rows(wk_s, wk_scales, range(ROWS))
        load_table(0)
        load_table(1)
        load_scale_rows(wv4_s, wv4_scales, range(1))

        nc.vector.tensor_copy(got_rows[:], tab_s[:].indirect(offsets[:]))
        got_s = tile("got_s", [P, PASSES, J], U8, tag="tab_s")
        span = ROWS * PASSES
        for q in (0, 2, 1, 3):
            nc.sync.dma_start(
                out=got_s[q * QUAD : q * QUAD + ROWS, :, :].bitcast(I32),
                in_=got_rows[COMPACT + q * span : COMPACT + (q + 1) * span, :].bitcast(I32),
            )
        load_words(wk_w, wk_words)
        load_wvd(1)
        load_rows(st_sb, st, 0)
        load_wv4_words(0)
        load_scale_rows(wv4_s, wv4_scales, range(1, ROWS))
        load_rows(st_sb, st, 1)
        load_rows(r_sb, rT, 0)
        load_wv4_words(1)
        load_rows(r_sb, rT, 1)

        wvd_w_all = tile("wvd_w", [P, PASSES * N], U32)
        wvd_s_all = tile("wvd_s", [P, PASSES * N], U8)
        wvd_w = [wvd_w_all[:, a * N : (a + 1) * N] for a in range(PASSES)]
        wvd_s = [wvd_s_all[:, a * N : (a + 1) * N] for a in range(PASSES)]
        grouped = {}

        def interleave(copy, a, n0, n1):
            piece = tile(f"grouped{a}_{n0}", [P, n1 - n0, PACK], BF16)
            grouped.setdefault((a, n0), piece)
            copy(
                out=piece[:].rearrange("p (c i) t -> p c t i", i=4),
                in_=wvd_raw[a][:, :, n0:n1].rearrange("p t (c i) -> p c t i", i=4),
            )

        def quantize(a, n0, n1):
            nc.vector.quantize_mx(
                out=wvd_w[a][:, n0:n1].bitcast(FP8X4),
                scales=wvd_s[a][:, n0:n1],
                in_=grouped[a, n0][:].rearrange("p n t -> p (n t)"),
            )

        halves = [slice(c * J // 2, (c + 1) * J // 2) for c in range(2)]
        whole = slice(0, J)
        ve0 = [psum.tile([P, J // 2], F32, name=f"ve0{c}", tag=f"ve0{c}") for c in range(2)]
        ke0 = psum.tile([P, J], F32, name="ke0")
        ke1 = psum.tile([P, J], F32, name="ke1", tag="ke1")
        ke = [[bank[:, cols] for cols in halves] for bank in (ke0, ke1)]

        def mx_pass(acc, cols, lhsT, lhsT_scale, a, start, stop):
            nc.tensor.matmul_mx(
                out=acc[:],
                lhsT=lhsT,
                lhsT_scale=lhsT_scale,
                rhs=got_w[a][:, cols].bitcast(FP8X4),
                rhs_scale=got_s[:, a, cols],
                start=start,
                stop=stop,
            )

        def wk_pass(acc, cols, a, h):
            codes = wk_w[:, a, 2 * h * P : 2 * (h + 1) * P].bitcast(FP4X4)
            mx_pass(acc, cols, codes, wk_s[:, a, h * P : (h + 1) * P], a, a == 0, a == PASSES - 1)

        def wv4_pass(acc, cols, a, h, stop):
            codes = wv4_w[h][:, a, :].bitcast(FP4X4)
            mx_pass(acc, cols, codes, wv4_s[:, a, h * P : (h + 1) * P], a, False, stop)

        def fp8_pass(acc, cols, a, h, start, stop):
            chans = slice(h * P, (h + 1) * P)
            mx_pass(acc, cols, wvd_w[a][:, chans].bitcast(FP8X4), wvd_s[a][:, chans], a, start, stop)

        gate = [tile(f"gate{h}", [P, J], F32) for h in range(HALVES)]

        def make_gate(h):
            for c in range(2):
                cols = slice(c * J // 2, (c + 1) * J // 2)
                logit = tile(f"logit{h}{c}", [P, J // 2], F32)
                nc.vector.tensor_tensor(logit[:], ke[h][c], st_sb[h][:, cols], MULT)
                nc.scalar.activation(gate[h][:, cols], logit[:], SIGMOID)

        for h in range(HALVES):
            interleave(nc.vector.tensor_copy, 0, h * P, (h + 1) * P)
        for h in range(HALVES):
            quantize(0, h * P, (h + 1) * P)
        for a in range(PASSES):
            nc.vector.tensor_copy(got_w[a][:], tab_w[a][:].indirect(offsets[:]))
        unread = psum.tile([NARROW, J], F32, name="unread")
        for i in range(3):
            nc.tensor.matmul_mx(
                out=unread[:],
                lhsT=wvd_w[0][:, 0:NARROW].bitcast(FP8X4),
                lhsT_scale=wvd_s[0][:, 0:NARROW],
                rhs=tab_w[0][:, 0:J].bitcast(FP8X4),
                rhs_scale=got_rows[:],
                start=True,
                stop=True,
            )
        for a in range(PASSES):
            wk_pass(ke0, whole, a, 0)
        for a in range(PASSES):
            wk_pass(ke1, whole, a, 1)
        interleave(nc.vector.tensor_copy, 1, 0, P)
        interleave(nc.vector.tensor_copy, 1, P, N)
        quantize(1, 0, P)
        make_gate(0)
        quantize(1, P, N)
        make_gate(1)
        def ve_group(bank, cols, h, wvd_last):
            fp8_pass(bank, cols, 0, h, True, False)
            if not wvd_last:
                fp8_pass(bank, cols, 1, h, False, False)
            for a in range(PASSES):
                wv4_pass(bank, cols, a, h, a == PASSES - 1 and not wvd_last)
            if wvd_last:
                fp8_pass(bank, cols, 1, h, False, True)

        gated = st_sb[1]
        for h, cuts in enumerate(((0, J // 2, J), (0, J // 2, J - LAST, J))):
            if h == 0:
                banks = ve0
            else:
                banks = [psum.tile([P, J // 2], F32, name=f"ve1{c}", tag=tag) for c, tag in enumerate(("ke1", "ve00"))]
            for c, cols in enumerate(halves):
                ve_group(banks[c], cols, h, (h, c) == (0, 1))
            for c, cols in enumerate(halves):
                nc.vector.tensor_tensor(gated[:, cols], banks[c][:], gate[h][:, cols], MULT)
            for j0, j1 in zip(cuts, cuts[1:]):
                res = tile(f"res{h}_{j0}", [P, j1 - j0], F32)
                nc.vector.tensor_tensor(
                    res[:], r_sb[h][:].indirect(offsets[:, j0 // 16 : j1 // 16]), gated[:, j0:j1], ADD
                )
                nc.sync.dma_start(out=out[h * P : (h + 1) * P, j0:j1], in_=res[:])
